import numpy as np
import ml_dtypes


def mxq(x, axis, fmt="e4m3"):
    dtype, down = {"e4m3": (ml_dtypes.float8_e4m3fn, 7), "e5m2": (ml_dtypes.float8_e5m2, 14)}[fmt]
    v = np.moveaxis(np.asarray(x, np.float32).astype(ml_dtypes.bfloat16).astype(np.float64), axis, -1)
    blocks = v.reshape(v.shape[:-1] + (-1, 32))
    amax = np.abs(blocks).max(-1, keepdims=True)
    byte = np.maximum(np.where(amax > 0, np.frexp(amax)[1] - 1 + 127, 0) - down, 1)
    scale = np.exp2(byte - 127.0)
    codes = (blocks / scale).astype(np.float32).astype(dtype).astype(np.float64)
    return np.moveaxis((codes * scale).reshape(v.shape), -1, axis)


WIDE = False


def mx_kscale(k):
    if not WIDE:
        return np.ones(k)
    levels = np.array([10, -10, 5, -5, 0])
    if k % 512:
        return np.exp2(np.random.permutation(np.resize(levels, k // 32))).repeat(32)
    a = np.empty((k // 512, 16))
    for p in range(k // 512):
        a[p, :8] = np.random.permutation(np.resize(levels, 8))
        for g in range(8):
            far = levels[np.abs(levels - a[p, g]) >= 10]
            a[p, g + 8] = far[np.random.randint(len(far))]
    return np.exp2(a.ravel()).repeat(32)


def f64(x):
    return np.asarray(x).astype(np.float64)


def striped(idx):
    return np.tile(idx.reshape(-1, 16).T, (8, 1)).astype(np.uint16)


def unstriped(offs):
    return offs[:16].T.reshape(-1).astype(np.int64)


E2M1 = np.array([0.0, 0.5, 1.0, 1.5, 2.0, 3.0, 4.0, 6.0, -0.0, -0.5, -1.0, -1.5, -2.0, -3.0, -4.0, -6.0])


def pack_fp4(w):
    k, n = w.shape
    w = f64(np.asarray(w, np.float32).astype(ml_dtypes.bfloat16)).reshape(k // 32, 32, n)
    amax = np.abs(w).max(1)
    mant, ex = np.frexp(amax / 6.0)
    byte = np.clip(np.where(amax > 0, np.where(mant > 0.5, ex, ex - 1) + 127, 1), 1, 254)
    scaled = (w * np.exp2(127.0 - byte)[:, None, :]).reshape(k, n).astype(np.float32)
    c = np.ascontiguousarray(scaled.reshape(k // 512, 128, 4, n).transpose(0, 1, 3, 2)).astype(ml_dtypes.float4_e2m1fn).view(np.uint8) & 0xF
    words = (c[..., 0::2] | (c[..., 1::2] << 4)).reshape(k // 512, 128, 2 * n)
    return np.ascontiguousarray(words), np.ascontiguousarray(byte.astype(np.uint8).reshape(k // 512, 16, n))


def unpack_fp4(words, scales):
    g, _, n = scales.shape
    words = np.ascontiguousarray(words).reshape(g, 128, n, 2)
    nib = np.empty((g, 128, n, 4), np.uint8)
    nib[..., 0::2] = words & 0xF
    nib[..., 1::2] = words >> 4
    vals = E2M1[nib] * np.repeat(np.exp2(scales.astype(np.float64) - 127.0), 8, axis=1)[..., None]
    return vals.transpose(0, 1, 3, 2).reshape(g * 512, n)


def planes(y):
    n, m = y.shape
    v = y.astype(np.float32).astype(ml_dtypes.bfloat16).astype(np.float64).reshape(n // 32, 32, m)
    top = np.abs(v).max(1)
    byte = np.clip(np.where(top > 0, np.frexp(top)[1] - 1 + 127 - 7, 1), 1, 254)
    codes = (v * np.exp2(127.0 - byte)[:, None, :]).reshape(n, m).astype(np.float32).astype(ml_dtypes.float8_e4m3fn).view(np.uint8)
    words = codes.reshape(n // 512, 128, 4, m).transpose(0, 1, 3, 2)
    return np.ascontiguousarray(words), np.ascontiguousarray(byte.astype(np.uint8).reshape(n // 512, 16, m))


K, T, N, U = 512, 1024, 512, 2048


def setup_inputs():
    n = np.random.standard_normal
    s = mx_kscale(K)[:, None]
    packed_xT = pack_fp4(n((K, T)) * s)
    return {
        "x_words": packed_xT[0],
        "x_scales": packed_xT[1],
        "mem": n((N, U)).astype(np.float32),
        "w1": (n((K, N)) / np.sqrt(K) / s).astype(np.float32),
        "slot": striped(np.random.permutation(U)[:T]),
    }


def reference(x_words, x_scales, mem, w1, slot):
    xq = unpack_fp4(x_words, x_scales)
    y = mxq(f64(w1), 0, "e4m3").T @ xq
    out = f64(mem).copy()
    out[:, unstriped(slot)] = np.minimum(f64(mem)[:, unstriped(slot)], y)
    return (out,) + planes(out)

@@ -1,0 +1,116 @@
+from contextlib import ExitStack
+
+import concourse.mybir as mybir
+
+K, T, N, U = 512, 1024, 512, 2048
+FLOPS = 2 * K * N * T
+
+F32 = mybir.dt.float32
+BF16 = mybir.dt.bfloat16
+I32 = mybir.dt.int32
+U32 = mybir.dt.uint32
+U16 = mybir.dt.uint16
+U8 = mybir.dt.uint8
+FP8X4 = mybir.dt.float8_e4m3fn_x4
+FP4X4 = mybir.dt.float4_e2m1fn_x4
+MIN = mybir.AluOpType.min
+
+P = 128
+PACK = 4
+BANK = 512
+
+CHUNKS = [(1536, 512, True), (0, 256, False), (1280, 256, True), (256, 256, False), (1152, 128, True),
+          (512, 256, False), (768, 256, False), (1024, 128, False)]
+WORD_STORES = [(1280, 768), (0, 512), (512, 512), (1024, 256)]
+
+
+def tile_picked_widxput_min_lo_kernel(tc, x_words, x_scales, mem, w1, slot, out_0, out_1, out_2):
+    nc = tc.nc
+    mem_rows = mem.rearrange("(p t) c -> p t c", t=PACK)
+    out_rows = out_0.rearrange("(p t) c -> p t c", t=PACK)
+    out_words = out_1[0].rearrange("p c r -> p (c r)").bitcast(I32)
+
+    with ExitStack() as ctx:
+        keep = ctx.enter_context(tc.tile_pool(name="keep", bufs=1))
+        ring = ctx.enter_context(tc.tile_pool(name="ring", bufs=2))
+        psum = ctx.enter_context(tc.psum_pool(name="psum", bufs=1))
+
+        w_raw = keep.tile([P, PACK, N], F32, name="w_raw")
+        nc.sync.dma_start(w_raw[:], w1.rearrange("(p j) c -> p j c", j=PACK))
+        store = [keep.tile([P, U], F32, name="store%d" % t) for t in range(PACK)]
+        nc.sync.dma_start(store[0][:], mem_rows[:, 0, :])
+        offsets = keep.tile([P, T // 16], U16, name="offsets")
+        nc.sync.dma_start(offsets[:], slot)
+        x_codes = keep.tile([P, 2 * T], U8, name="x_codes", align_bytes=64)
+        nc.sync.dma_start(x_codes[:].bitcast(I32), x_words[0].bitcast(I32))
+        x_plane = keep.tile([P, T], U8, name="x_plane", align_bytes=64)
+        nc.vector.memset(x_plane[:].bitcast(I32), 0)
+        for q in range(4):
+            nc.scalar.dma_start(x_plane[32 * q : 32 * q + 4, :].bitcast(I32), x_scales[0, 4 * q : 4 * q + 4, :].bitcast(I32))
+        for t in range(1, PACK):
+            nc.sync.dma_start(store[t][:], mem_rows[:, t, :])
+
+        w_by_t = w_raw[:].rearrange("p j (m t) -> p m t j", t=PACK)
+        w_rounded = [keep.tile([P, 2, P, PACK], BF16, name="w_rounded%d" % u, align_bytes=64) for u in range(2)]
+        w_codes = [keep.tile([P, 2 * P], U32, name="w_codes%d" % u, align_bytes=64) for u in range(2)]
+        w_plane = [keep.tile([P, 2 * P], U8, name="w_plane%d" % u, align_bytes=64) for u in range(2)]
+        banks = [[psum.tile([P, BANK], F32, name="bank%d_%d" % (t, h)) for h in range(T // BANK)] for t in range(PACK)]
+
+        def project(u):
+            nc.vector.quantize_mx(out=w_codes[u][:].bitcast(FP8X4), scales=w_plane[u][:], in_=w_rounded[u][:].rearrange("p t m j -> p (t m j)"))
+            for e in range(2):
+                for h in range(T // BANK):
+                    nc.tensor.matmul_mx(
+                        out=banks[2 * u + e][h][:],
+                        lhsT=w_codes[u][:, P * e : P * (e + 1)].bitcast(FP8X4),
+                        lhsT_scale=w_plane[u][:, P * e : P * (e + 1)],
+                        rhs=x_codes[:, 2 * BANK * h : 2 * BANK * (h + 1)].bitcast(FP4X4),
+                        rhs_scale=x_plane[:, BANK * h : BANK * (h + 1)],
+                        start=True,
+                        stop=True,
+                    )
+
+        def look_up(t):
+            old = [ring.tile([P, BANK], F32, name="old%d" % h) for h in range(T // BANK)]
+            for h in range(T // BANK):
+                nc.vector.tensor_copy(old[h][:], store[t][:].indirect(offsets[:, BANK // 16 * h : BANK // 16 * (h + 1)]))
+            return old
+
+        rounded_out = [keep.tile([P, width, PACK], BF16, name="rounded%d" % c, align_bytes=64) for c, (first, width, on_vector) in enumerate(CHUNKS)]
+        words = keep.tile([P, U], U32, name="words", align_bytes=64)
+        plane = keep.tile([P, U], U8, name="plane", align_bytes=64)
+
+        nc.vector.tensor_copy(w_rounded[0][:].rearrange("p t m j -> p m t j"), w_by_t[:, :, 0:2, :])
+        nc.scalar.copy(w_rounded[1][:].rearrange("p t m j -> p m t j"), w_by_t[:, :, 2:4, :])
+        project(0)
+        project(1)
+        old = look_up(0)
+
+        for t in range(PACK):
+            new = ring.tile([P, T], F32, name="new")
+            for h in range(T // BANK):
+                nc.vector.tensor_tensor(new[:, BANK * h : BANK * (h + 1)], old[h][:], banks[t][h][:], MIN)
+            if t + 1 < PACK:
+                old = look_up(t + 1)
+            nc.vector.tensor_copy(store[t][:].indirect(offsets[:]), new[:])
+            nc.sync.dma_start(out_rows[:, t, :], store[t][:])
+            last = t == PACK - 1
+            for c, (first, width, on_vector) in enumerate(CHUNKS):
+                if last and on_vector:
+                    nc.vector.tensor_copy(rounded_out[c][:, :, t], store[t][:, first : first + width])
+            for c, (first, width, on_vector) in enumerate(CHUNKS):
+                if t == PACK - 2 and on_vector:
+                    nc.scalar.copy(rounded_out[c][:, :, t:], store[t][:, first : first + width].unsqueeze(2).to_broadcast([P, width, 2]))
+                elif not (last and on_vector):
+                    nc.scalar.copy(rounded_out[c][:, :, t], store[t][:, first : first + width])
+
+        for c, (first, width, on_vector) in enumerate(CHUNKS):
+            nc.vector.quantize_mx(
+                out=words[:, first : first + width].bitcast(FP8X4),
+                scales=plane[:, first : first + width],
+                in_=rounded_out[c][:].rearrange("p c t -> p (c t)"),
+            )
+        for first, width in WORD_STORES:
+            nc.sync.dma_start(out_words[:, first : first + width], words[:, first : first + width].bitcast(I32))
+        for q in range(4):
+            nc.scalar.dma_start(out_2[0, 4 * q : 4 * q + 4, :].bitcast(I32), plane[32 * q : 32 * q + 4, :].bitcast(I32))

@@ -18,10 +18,11 @@ MIN = mybir.AluOpType.min
 P = 128
 PACK = 4
 BANK = 512
+GROUP = 1024
 
-CHUNKS = [(1536, 512, True), (0, 256, False), (1280, 256, True), (256, 256, False), (1152, 128, True),
+CHUNKS = [(1536, 512, True), (0, 256, False), (1280, 256, True), (1152, 128, True), (256, 256, False),
           (512, 256, False), (768, 256, False), (1024, 128, False)]
-WORD_STORES = [(1280, 768), (0, 512), (512, 512), (1024, 256)]
+WORD_STORES = [(1536, 512), (1152, 384), (0, 512), (512, 512), (1024, 128)]
 
 
 def tile_picked_widxput_min_lo_kernel(tc, x_words, x_scales, mem, w1, slot, out_0, out_1, out_2):
@@ -37,10 +38,10 @@ def tile_picked_widxput_min_lo_kernel(tc, x_words, x_scales, mem, w1, slot, out_
 
         w_raw = keep.tile([P, PACK, N], F32, name="w_raw")
         nc.sync.dma_start(w_raw[:], w1.rearrange("(p j) c -> p j c", j=PACK))
-        store = [keep.tile([P, U], F32, name="store%d" % t) for t in range(PACK)]
-        nc.sync.dma_start(store[0][:], mem_rows[:, 0, :])
         offsets = keep.tile([P, T // 16], U16, name="offsets")
         nc.sync.dma_start(offsets[:], slot)
+        store = [keep.tile([P, U], F32, name="store%d" % t) for t in range(PACK)]
+        nc.sync.dma_start(store[0][:], mem_rows[:, 0, :])
         x_codes = keep.tile([P, 2 * T], U8, name="x_codes", align_bytes=64)
         nc.sync.dma_start(x_codes[:].bitcast(I32), x_words[0].bitcast(I32))
         x_plane = keep.tile([P, T], U8, name="x_plane", align_bytes=64)
@@ -78,7 +79,7 @@ def tile_picked_widxput_min_lo_kernel(tc, x_words, x_scales, mem, w1, slot, out_
 
         rounded_out = [keep.tile([P, width, PACK], BF16, name="rounded%d" % c, align_bytes=64) for c, (first, width, on_vector) in enumerate(CHUNKS)]
         words = keep.tile([P, U], U32, name="words", align_bytes=64)
-        plane = keep.tile([P, U], U8, name="plane", align_bytes=64)
+        plane = keep.tile([P, GROUP], U8, name="plane", align_bytes=64)
 
         nc.vector.tensor_copy(w_rounded[0][:].rearrange("p t m j -> p m t j"), w_by_t[:, :, 0:2, :])
         nc.scalar.copy(w_rounded[1][:].rearrange("p t m j -> p m t j"), w_by_t[:, :, 2:4, :])
@@ -105,12 +106,17 @@ def tile_picked_widxput_min_lo_kernel(tc, x_words, x_scales, mem, w1, slot, out_
                     nc.scalar.copy(rounded_out[c][:, :, t], store[t][:, first : first + width])
 
         for c, (first, width, on_vector) in enumerate(CHUNKS):
+            group, col = divmod(first, GROUP)
             nc.vector.quantize_mx(
                 out=words[:, first : first + width].bitcast(FP8X4),
-                scales=plane[:, first : first + width],
+                scales=plane[4 * group :, col : col + width],
                 in_=rounded_out[c][:].rearrange("p c t -> p (c t)"),
             )
         for first, width in WORD_STORES:
             nc.sync.dma_start(out_words[:, first : first + width], words[:, first : first + width].bitcast(I32))
         for q in range(4):
-            nc.scalar.dma_start(out_2[0, 4 * q : 4 * q + 4, :].bitcast(I32), plane[32 * q : 32 * q + 4, :].bitcast(I32))
+            queue = nc.sync if q < 2 else nc.scalar
+            queue.dma_start(
+                out_2[0, 4 * q : 4 * q + 4, :].bitcast(I32).rearrange("r (g c) -> g r c", g=U // GROUP),
+                plane[32 * q : 32 * q + 4 * (U // GROUP), :].bitcast(I32),
+            )

@@ -18,11 +18,11 @@ MIN = mybir.AluOpType.min
 P = 128
 PACK = 4
 BANK = 512
-GROUP = 1024
+GROUP = 512
 
-CHUNKS = [(1536, 512, True), (0, 256, False), (1280, 256, True), (1152, 128, True), (256, 256, False),
-          (512, 256, False), (768, 256, False), (1024, 128, False)]
-WORD_STORES = [(1536, 512), (1152, 384), (0, 512), (512, 512), (1024, 128)]
+CHUNKS = [(0, 256, True), (256, 256, True), (512, 256, False), (768, 256, False), (1024, 128, True),
+          (1152, 256, True), (1408, 128, False), (1536, 256, False), (1792, 256, False)]
+WORD_STORES = [(0, 768), (768, 640), (1408, 384), (1792, 256)]
 
 
 def tile_picked_widxput_min_lo_kernel(tc, x_words, x_scales, mem, w1, slot, out_0, out_1, out_2):
@@ -42,12 +42,12 @@ def tile_picked_widxput_min_lo_kernel(tc, x_words, x_scales, mem, w1, slot, out_
         nc.sync.dma_start(offsets[:], slot)
         store = [keep.tile([P, U], F32, name="store%d" % t) for t in range(PACK)]
         nc.sync.dma_start(store[0][:], mem_rows[:, 0, :])
-        x_codes = keep.tile([P, 2 * T], U8, name="x_codes", align_bytes=64)
-        nc.sync.dma_start(x_codes[:].bitcast(I32), x_words[0].bitcast(I32))
         x_plane = keep.tile([P, T], U8, name="x_plane", align_bytes=64)
         nc.vector.memset(x_plane[:].bitcast(I32), 0)
         for q in range(4):
-            nc.scalar.dma_start(x_plane[32 * q : 32 * q + 4, :].bitcast(I32), x_scales[0, 4 * q : 4 * q + 4, :].bitcast(I32))
+            nc.sync.dma_start(x_plane[32 * q : 32 * q + 4, :].bitcast(I32), x_scales[0, 4 * q : 4 * q + 4, :].bitcast(I32))
+        x_codes = keep.tile([P, 2 * T], U8, name="x_codes", align_bytes=64)
+        nc.sync.dma_start(x_codes[:].bitcast(I32), x_words[0].bitcast(I32))
         for t in range(1, PACK):
             nc.sync.dma_start(store[t][:], mem_rows[:, t, :])
 
@@ -115,7 +115,7 @@ def tile_picked_widxput_min_lo_kernel(tc, x_words, x_scales, mem, w1, slot, out_
         for first, width in WORD_STORES:
             nc.sync.dma_start(out_words[:, first : first + width], words[:, first : first + width].bitcast(I32))
         for q in range(4):
-            queue = nc.sync if q < 2 else nc.scalar
+            queue = nc.scalar
             queue.dma_start(
                 out_2[0, 4 * q : 4 * q + 4, :].bitcast(I32).rearrange("r (g c) -> g r c", g=U // GROUP),
                 plane[32 * q : 32 * q + 4 * (U // GROUP), :].bitcast(I32),

@@ -19,6 +19,7 @@ P = 128
 PACK = 4
 BANK = 512
 GROUP = 512
+ORDER = (0, 2, 1, 3)
 
 CHUNKS = [(0, 256, True), (256, 256, True), (512, 256, False), (768, 256, False), (1024, 128, True),
           (1152, 256, True), (1408, 128, False), (1536, 256, False), (1792, 256, False)]
@@ -48,52 +49,56 @@ def tile_picked_widxput_min_lo_kernel(tc, x_words, x_scales, mem, w1, slot, out_
             nc.sync.dma_start(x_plane[32 * q : 32 * q + 4, :].bitcast(I32), x_scales[0, 4 * q : 4 * q + 4, :].bitcast(I32))
         x_codes = keep.tile([P, 2 * T], U8, name="x_codes", align_bytes=64)
         nc.sync.dma_start(x_codes[:].bitcast(I32), x_words[0].bitcast(I32))
-        for t in range(1, PACK):
+        for t in ORDER[1:]:
             nc.sync.dma_start(store[t][:], mem_rows[:, t, :])
 
         w_by_t = w_raw[:].rearrange("p j (m t) -> p m t j", t=PACK)
-        w_rounded = [keep.tile([P, 2, P, PACK], BF16, name="w_rounded%d" % u, align_bytes=64) for u in range(2)]
-        w_codes = [keep.tile([P, 2 * P], U32, name="w_codes%d" % u, align_bytes=64) for u in range(2)]
-        w_plane = [keep.tile([P, 2 * P], U8, name="w_plane%d" % u, align_bytes=64) for u in range(2)]
+        w_vector = keep.tile([P, PACK - 1, P, PACK], BF16, name="w_vector", align_bytes=64)
+        w_scalar = keep.tile([P, 1, P, PACK], BF16, name="w_scalar", align_bytes=64)
+        w_codes = keep.tile([P, N], U32, name="w_codes", align_bytes=64)
+        w_plane = keep.tile([P, N], U8, name="w_plane", align_bytes=64)
         banks = [[psum.tile([P, BANK], F32, name="bank%d_%d" % (t, h)) for h in range(T // BANK)] for t in range(PACK)]
 
-        def project(u):
-            nc.vector.quantize_mx(out=w_codes[u][:].bitcast(FP8X4), scales=w_plane[u][:], in_=w_rounded[u][:].rearrange("p t m j -> p (t m j)"))
-            for e in range(2):
+        def project(first, count, rounded):
+            cols = slice(P * first, P * (first + count))
+            nc.vector.quantize_mx(out=w_codes[:, cols].bitcast(FP8X4), scales=w_plane[:, cols], in_=rounded.rearrange("p t m j -> p (t m j)"))
+            for t in range(first, first + count):
                 for h in range(T // BANK):
                     nc.tensor.matmul_mx(
-                        out=banks[2 * u + e][h][:],
-                        lhsT=w_codes[u][:, P * e : P * (e + 1)].bitcast(FP8X4),
-                        lhsT_scale=w_plane[u][:, P * e : P * (e + 1)],
+                        out=banks[t][h][:],
+                        lhsT=w_codes[:, P * t : P * (t + 1)].bitcast(FP8X4),
+                        lhsT_scale=w_plane[:, P * t : P * (t + 1)],
                         rhs=x_codes[:, 2 * BANK * h : 2 * BANK * (h + 1)].bitcast(FP4X4),
                         rhs_scale=x_plane[:, BANK * h : BANK * (h + 1)],
                         start=True,
                         stop=True,
                     )
 
-        def look_up(t):
-            old = [ring.tile([P, BANK], F32, name="old%d" % h) for h in range(T // BANK)]
-            for h in range(T // BANK):
-                nc.vector.tensor_copy(old[h][:], store[t][:].indirect(offsets[:, BANK // 16 * h : BANK // 16 * (h + 1)]))
+        def look_up(t, h):
+            old = ring.tile([P, BANK], F32, name="old%d" % h)
+            nc.vector.tensor_copy(old[:], store[t][:].indirect(offsets[:, BANK // 16 * h : BANK // 16 * (h + 1)]))
             return old
 
         rounded_out = [keep.tile([P, width, PACK], BF16, name="rounded%d" % c, align_bytes=64) for c, (first, width, on_vector) in enumerate(CHUNKS)]
         words = keep.tile([P, U], U32, name="words", align_bytes=64)
         plane = keep.tile([P, GROUP], U8, name="plane", align_bytes=64)
 
-        nc.vector.tensor_copy(w_rounded[0][:].rearrange("p t m j -> p m t j"), w_by_t[:, :, 0:2, :])
-        nc.scalar.copy(w_rounded[1][:].rearrange("p t m j -> p m t j"), w_by_t[:, :, 2:4, :])
-        project(0)
-        project(1)
-        old = look_up(0)
+        nc.vector.tensor_copy(w_vector[:].rearrange("p t m j -> p m t j"), w_by_t[:, :, : PACK - 1, :])
+        nc.scalar.copy(w_scalar[:].rearrange("p t m j -> p m t j"), w_by_t[:, :, PACK - 1 :, :])
+        project(0, 2, w_vector[:, 0:2, :, :])
+        project(2, 1, w_vector[:, 2:3, :, :])
+        project(3, 1, w_scalar[:])
+        old = [look_up(ORDER[0], h) for h in range(T // BANK)]
 
-        for t in range(PACK):
+        for step, t in enumerate(ORDER):
             new = ring.tile([P, T], F32, name="new")
             for h in range(T // BANK):
                 nc.vector.tensor_tensor(new[:, BANK * h : BANK * (h + 1)], old[h][:], banks[t][h][:], MIN)
-            if t + 1 < PACK:
-                old = look_up(t + 1)
+            if step + 1 < PACK:
+                old = [look_up(ORDER[step + 1], 0)]
             nc.vector.tensor_copy(store[t][:].indirect(offsets[:]), new[:])
+            if step + 1 < PACK:
+                old.append(look_up(ORDER[step + 1], 1))
             nc.sync.dma_start(out_rows[:, t, :], store[t][:])
             last = t == PACK - 1
             for c, (first, width, on_vector) in enumerate(CHUNKS):

@@ -13,13 +13,16 @@ U16 = mybir.dt.uint16
 U8 = mybir.dt.uint8
 FP8X4 = mybir.dt.float8_e4m3fn_x4
 FP4X4 = mybir.dt.float4_e2m1fn_x4
-MIN = mybir.AluOpType.min
+ALU = mybir.AluOpType
+ACT = mybir.ActivationFunctionType
 
 P = 128
 PACK = 4
 BANK = 512
 GROUP = 512
 ORDER = (0, 2, 1, 3)
+POOL_SHARE = (256,512,640,768)
+POOL_ROUNDS = 640
 
 CHUNKS = [(0, 256, True), (256, 256, True), (512, 256, False), (768, 256, False), (1024, 128, True),
           (1152, 256, True), (1408, 128, False), (1536, 256, False), (1792, 256, False)]
@@ -34,94 +37,135 @@ def tile_picked_widxput_min_lo_kernel(tc, x_words, x_scales, mem, w1, slot, out_
 
     with ExitStack() as ctx:
         keep = ctx.enter_context(tc.tile_pool(name="keep", bufs=1))
-        ring = ctx.enter_context(tc.tile_pool(name="ring", bufs=2))
+        shared = ctx.enter_context(tc.tile_pool(name="shared", bufs=1))
         psum = ctx.enter_context(tc.psum_pool(name="psum", bufs=1))
 
-        w_raw = keep.tile([P, PACK, N], F32, name="w_raw")
-        nc.sync.dma_start(w_raw[:], w1.rearrange("(p j) c -> p j c", j=PACK))
         offsets = keep.tile([P, T // 16], U16, name="offsets")
-        nc.sync.dma_start(offsets[:], slot)
         store = [keep.tile([P, U], F32, name="store%d" % t) for t in range(PACK)]
-        nc.sync.dma_start(store[0][:], mem_rows[:, 0, :])
+        w_raw = keep.tile([P, PACK, N], F32, name="w_raw")
         x_plane = keep.tile([P, T], U8, name="x_plane", align_bytes=64)
-        nc.vector.memset(x_plane[:].bitcast(I32), 0)
-        for q in range(4):
-            nc.sync.dma_start(x_plane[32 * q : 32 * q + 4, :].bitcast(I32), x_scales[0, 4 * q : 4 * q + 4, :].bitcast(I32))
         x_codes = keep.tile([P, 2 * T], U8, name="x_codes", align_bytes=64)
+        nc.vector.memset(x_plane[:].bitcast(I32), 0)
+        nc.sync.dma_start(offsets[:], slot)
+        for t in ORDER[:2]:
+            nc.sync.dma_start(store[t][:], mem_rows[:, t, :])
+        nc.sync.dma_start(w_raw[:], w1.rearrange("(p j) c -> p j c", j=PACK))
         nc.sync.dma_start(x_codes[:].bitcast(I32), x_words[0].bitcast(I32))
-        for t in ORDER[1:]:
+        for q in range(4):
+            nc.scalar.dma_start(x_plane[32 * q : 32 * q + 4, :].bitcast(I32), x_scales[0, 4 * q : 4 * q + 4, :].bitcast(I32))
+        for t in ORDER[2:]:
             nc.sync.dma_start(store[t][:], mem_rows[:, t, :])
 
-        w_by_t = w_raw[:].rearrange("p j (m t) -> p m t j", t=PACK)
-        w_vector = keep.tile([P, PACK - 1, P, PACK], BF16, name="w_vector", align_bytes=64)
-        w_scalar = keep.tile([P, 1, P, PACK], BF16, name="w_scalar", align_bytes=64)
+        w_by_t = w_raw[:].rearrange("p j (m t) -> p t m j", t=PACK)
+        w_round = [keep.tile([P, P, PACK], BF16, name="w_round%d" % t, align_bytes=64) for t in range(PACK)]
         w_codes = keep.tile([P, N], U32, name="w_codes", align_bytes=64)
         w_plane = keep.tile([P, N], U8, name="w_plane", align_bytes=64)
         banks = [[psum.tile([P, BANK], F32, name="bank%d_%d" % (t, h)) for h in range(T // BANK)] for t in range(PACK)]
 
-        def project(first, count, rounded):
-            cols = slice(P * first, P * (first + count))
-            nc.vector.quantize_mx(out=w_codes[:, cols].bitcast(FP8X4), scales=w_plane[:, cols], in_=rounded.rearrange("p t m j -> p (t m j)"))
-            for t in range(first, first + count):
-                for h in range(T // BANK):
-                    nc.tensor.matmul_mx(
-                        out=banks[t][h][:],
-                        lhsT=w_codes[:, P * t : P * (t + 1)].bitcast(FP8X4),
-                        lhsT_scale=w_plane[:, P * t : P * (t + 1)],
-                        rhs=x_codes[:, 2 * BANK * h : 2 * BANK * (h + 1)].bitcast(FP4X4),
-                        rhs_scale=x_plane[:, BANK * h : BANK * (h + 1)],
-                        start=True,
-                        stop=True,
-                    )
+        def project(t):
+            cols = slice(P * t, P * (t + 1))
+            nc.vector.quantize_mx(out=w_codes[:, cols].bitcast(FP8X4), scales=w_plane[:, cols], in_=w_round[t][:].rearrange("p m j -> p (m j)"))
+            for h in range(T // BANK):
+                nc.tensor.matmul_mx(
+                    out=banks[t][h][:],
+                    lhsT=w_codes[:, cols].bitcast(FP8X4),
+                    lhsT_scale=w_plane[:, cols],
+                    rhs=x_codes[:, 2 * BANK * h : 2 * BANK * (h + 1)].bitcast(FP4X4),
+                    rhs_scale=x_plane[:, BANK * h : BANK * (h + 1)],
+                    start=True,
+                    stop=True,
+                )
 
-        def look_up(t, h):
-            old = ring.tile([P, BANK], F32, name="old%d" % h)
-            nc.vector.tensor_copy(old[:], store[t][:].indirect(offsets[:, BANK // 16 * h : BANK // 16 * (h + 1)]))
-            return old
+        signs = shared.tile([P, U * PACK], BF16, name="signs", align_bytes=64, offset=0)
+        share = dict(zip(ORDER, POOL_SHARE))
+        old = [keep.tile([P, T], F32, name="old%d" % t) for t in range(PACK)]
+        new = [keep.tile([P, T], F32, name="new%d" % t) for t in range(PACK)]
+        y = [keep.tile([P, share[t]], F32, name="y%d" % t) for t in range(PACK)]
+        keep_old = [keep.tile([P, share[t]], F32, name="keep_old%d" % t) for t in range(PACK)]
+        take_new = [keep.tile([P, share[t]], F32, name="take_new%d" % t) for t in range(PACK)]
 
-        rounded_out = [keep.tile([P, width, PACK], BF16, name="rounded%d" % c, align_bytes=64) for c, (first, width, on_vector) in enumerate(CHUNKS)]
+        def bank_pieces(first, end):
+            return [(h, max(first, BANK * h), min(end, BANK * (h + 1))) for h in range(T // BANK) if max(first, BANK * h) < min(end, BANK * (h + 1))]
+
+        def look_up(t):
+            nc.vector.tensor_copy(old[t][:], store[t][:].indirect(offsets[:]))
+
+        def smaller_on_vector(t):
+            for h, a, b in bank_pieces(0, T - share[t]):
+                nc.vector.tensor_tensor(new[t][:, a:b], old[t][:, a:b], banks[t][h][:, a - BANK * h : b - BANK * h], ALU.min)
+
+        def fetch_y(t):
+            first = T - share[t]
+            for h, a, b in bank_pieces(first, T):
+                nc.scalar.copy(y[t][:, a - first : b - first], banks[t][h][:, a - BANK * h : b - BANK * h])
+
+        def compare(t):
+            first = T - share[t]
+            gap = keep.tile([P, share[t]], F32, name={ORDER[2]: "keep_old%d" % ORDER[0], ORDER[3]: "take_new%d" % ORDER[0]}.get(t, "gap%d" % t))
+            side = signs[:, U * t : U * t + share[t]]
+            nc.gpsimd.tensor_tensor(gap[:], old[t][:, first:], y[t][:], ALU.subtract)
+            nc.scalar.activation(side, gap[:], ACT.Sign)
+            nc.scalar.activation(keep_old[t][:], side, ACT.Copy, scale=-0.5, bias=0.5)
+            nc.scalar.activation(take_new[t][:], side, ACT.Copy, scale=0.5, bias=0.5)
+
+        def choose(t):
+            first = T - share[t]
+            nc.gpsimd.tensor_tensor(keep_old[t][:], keep_old[t][:], old[t][:, first:], ALU.mult)
+            nc.gpsimd.tensor_tensor(take_new[t][:], take_new[t][:], y[t][:], ALU.mult)
+            nc.gpsimd.tensor_tensor(new[t][:, first:], keep_old[t][:], take_new[t][:], ALU.add)
+
+        rounded = [shared.tile([P, width, PACK], BF16, name="rounded%d" % c, align_bytes=64, offset=2 * PACK * first) for c, (first, width, on_vector) in enumerate(CHUNKS)]
         words = keep.tile([P, U], U32, name="words", align_bytes=64)
         plane = keep.tile([P, GROUP], U8, name="plane", align_bytes=64)
 
-        nc.vector.tensor_copy(w_vector[:].rearrange("p t m j -> p m t j"), w_by_t[:, :, : PACK - 1, :])
-        nc.scalar.copy(w_scalar[:].rearrange("p t m j -> p m t j"), w_by_t[:, :, PACK - 1 :, :])
-        project(0, 2, w_vector[:, 0:2, :, :])
-        project(2, 1, w_vector[:, 2:3, :, :])
-        project(3, 1, w_scalar[:])
-        old = [look_up(ORDER[0], h) for h in range(T // BANK)]
-
+        look_up(ORDER[0])
+        look_up(ORDER[1])
         for step, t in enumerate(ORDER):
-            new = ring.tile([P, T], F32, name="new")
-            for h in range(T // BANK):
-                nc.vector.tensor_tensor(new[:, BANK * h : BANK * (h + 1)], old[h][:], banks[t][h][:], MIN)
-            if step + 1 < PACK:
-                old = [look_up(ORDER[step + 1], 0)]
-            nc.vector.tensor_copy(store[t][:].indirect(offsets[:]), new[:])
-            if step + 1 < PACK:
-                old.append(look_up(ORDER[step + 1], 1))
+            if step == 1:
+                nc.vector.tensor_copy(w_round[t][:], w_by_t[:, t, :, :])
+            else:
+                nc.scalar.copy(w_round[t][:], w_by_t[:, t, :, :])
+        for t in ORDER:
+            project(t)
+            fetch_y(t)
+        for t in ORDER[:2]:
+            compare(t)
+            smaller_on_vector(t)
+        choose(ORDER[0])
+        for t in ORDER[2:]:
+            look_up(t)
+            compare(t)
+        for t in ORDER[2:]:
+            smaller_on_vector(t)
+        for t in ORDER[1:]:
+            choose(t)
+
+        for t in ORDER:
+            nc.vector.tensor_copy(store[t][:].indirect(offsets[:]), new[t][:])
             nc.sync.dma_start(out_rows[:, t, :], store[t][:])
-            last = t == PACK - 1
             for c, (first, width, on_vector) in enumerate(CHUNKS):
-                if last and on_vector:
-                    nc.vector.tensor_copy(rounded_out[c][:, :, t], store[t][:, first : first + width])
+                if t == 3 and on_vector:
+                    nc.vector.tensor_copy(rounded[c][:, :, t], store[t][:, first : first + width])
             for c, (first, width, on_vector) in enumerate(CHUNKS):
-                if t == PACK - 2 and on_vector:
-                    nc.scalar.copy(rounded_out[c][:, :, t:], store[t][:, first : first + width].unsqueeze(2).to_broadcast([P, width, 2]))
-                elif not (last and on_vector):
-                    nc.scalar.copy(rounded_out[c][:, :, t], store[t][:, first : first + width])
+                values = store[t][:, first : first + width]
+                if t % 2 == 0:
+                    nc.scalar.copy(rounded[c][:, :, t : t + 2], values.unsqueeze(2).to_broadcast([P, width, 2]))
+                elif t == 1 and first >= U - POOL_ROUNDS:
+                    nc.gpsimd.tensor_scalar(rounded[c][:, :, t], values, 1.0, -0.0, ALU.mult, ALU.add)
+                elif not (t == 3 and on_vector):
+                    nc.scalar.copy(rounded[c][:, :, t], values)
 
         for c, (first, width, on_vector) in enumerate(CHUNKS):
             group, col = divmod(first, GROUP)
             nc.vector.quantize_mx(
                 out=words[:, first : first + width].bitcast(FP8X4),
                 scales=plane[4 * group :, col : col + width],
-                in_=rounded_out[c][:].rearrange("p c t -> p (c t)"),
+                in_=rounded[c][:].rearrange("p c t -> p (c t)"),
             )
         for first, width in WORD_STORES:
             nc.sync.dma_start(out_words[:, first : first + width], words[:, first : first + width].bitcast(I32))
         for q in range(4):
-            queue = nc.scalar
-            queue.dma_start(
+            nc.scalar.dma_start(
                 out_2[0, 4 * q : 4 * q + 4, :].bitcast(I32).rearrange("r (g c) -> g r c", g=U // GROUP),
                 plane[32 * q : 32 * q + 4 * (U // GROUP), :].bitcast(I32),
             )

@@ -21,7 +21,7 @@ PACK = 4
 BANK = 512
 GROUP = 512
 ORDER = (0, 2, 1, 3)
-POOL_SHARE = (256,512,640,768)
+POOL_SHARE = (0,256,704,896)
 POOL_ROUNDS = 640
 
 CHUNKS = [(0, 256, True), (256, 256, True), (512, 256, False), (768, 256, False), (1024, 128, True),
@@ -49,12 +49,12 @@ def tile_picked_widxput_min_lo_kernel(tc, x_words, x_scales, mem, w1, slot, out_
         nc.sync.dma_start(offsets[:], slot)
         for t in ORDER[:2]:
             nc.sync.dma_start(store[t][:], mem_rows[:, t, :])
-        nc.sync.dma_start(w_raw[:], w1.rearrange("(p j) c -> p j c", j=PACK))
-        nc.sync.dma_start(x_codes[:].bitcast(I32), x_words[0].bitcast(I32))
         for q in range(4):
-            nc.scalar.dma_start(x_plane[32 * q : 32 * q + 4, :].bitcast(I32), x_scales[0, 4 * q : 4 * q + 4, :].bitcast(I32))
+            nc.sync.dma_start(x_plane[32 * q : 32 * q + 4, :].bitcast(I32), x_scales[0, 4 * q : 4 * q + 4, :].bitcast(I32))
         for t in ORDER[2:]:
             nc.sync.dma_start(store[t][:], mem_rows[:, t, :])
+        nc.sync.dma_start(w_raw[:], w1.rearrange("(p j) c -> p j c", j=PACK))
+        nc.sync.dma_start(x_codes[:].bitcast(I32), x_words[0].bitcast(I32))
 
         w_by_t = w_raw[:].rearrange("p j (m t) -> p t m j", t=PACK)
         w_round = [keep.tile([P, P, PACK], BF16, name="w_round%d" % t, align_bytes=64) for t in range(PACK)]
@@ -80,9 +80,9 @@ def tile_picked_widxput_min_lo_kernel(tc, x_words, x_scales, mem, w1, slot, out_
         share = dict(zip(ORDER, POOL_SHARE))
         old = [keep.tile([P, T], F32, name="old%d" % t) for t in range(PACK)]
         new = [keep.tile([P, T], F32, name="new%d" % t) for t in range(PACK)]
-        y = [keep.tile([P, share[t]], F32, name="y%d" % t) for t in range(PACK)]
-        keep_old = [keep.tile([P, share[t]], F32, name="keep_old%d" % t) for t in range(PACK)]
-        take_new = [keep.tile([P, share[t]], F32, name="take_new%d" % t) for t in range(PACK)]
+        y = {t: keep.tile([P, share[t]], F32, name="y%d" % t) for t in ORDER[1:]}
+        keep_old = {t: keep.tile([P, share[t]], F32, name="keep_old%d" % t) for t in ORDER[1:]}
+        take_new = {t: keep.tile([P, share[t]], F32, name="take_new%d" % t) for t in ORDER[1:]}
 
         def bank_pieces(first, end):
             return [(h, max(first, BANK * h), min(end, BANK * (h + 1))) for h in range(T // BANK) if max(first, BANK * h) < min(end, BANK * (h + 1))]
@@ -101,7 +101,7 @@ def tile_picked_widxput_min_lo_kernel(tc, x_words, x_scales, mem, w1, slot, out_
 
         def compare(t):
             first = T - share[t]
-            gap = keep.tile([P, share[t]], F32, name={ORDER[2]: "keep_old%d" % ORDER[0], ORDER[3]: "take_new%d" % ORDER[0]}.get(t, "gap%d" % t))
+            gap = keep.tile([P, share[t]], F32, name="gap%d" % t)
             side = signs[:, U * t : U * t + share[t]]
             nc.gpsimd.tensor_tensor(gap[:], old[t][:, first:], y[t][:], ALU.subtract)
             nc.scalar.activation(side, gap[:], ACT.Sign)
@@ -118,8 +118,8 @@ def tile_picked_widxput_min_lo_kernel(tc, x_words, x_scales, mem, w1, slot, out_
         words = keep.tile([P, U], U32, name="words", align_bytes=64)
         plane = keep.tile([P, GROUP], U8, name="plane", align_bytes=64)
 
-        look_up(ORDER[0])
-        look_up(ORDER[1])
+        for t in ORDER:
+            look_up(t)
         for step, t in enumerate(ORDER):
             if step == 1:
                 nc.vector.tensor_copy(w_round[t][:], w_by_t[:, t, :, :])
@@ -127,16 +127,12 @@ def tile_picked_widxput_min_lo_kernel(tc, x_words, x_scales, mem, w1, slot, out_
                 nc.scalar.copy(w_round[t][:], w_by_t[:, t, :, :])
         for t in ORDER:
             project(t)
+        for t in ORDER[1:]:
             fetch_y(t)
-        for t in ORDER[:2]:
-            compare(t)
+        for t in ORDER:
             smaller_on_vector(t)
-        choose(ORDER[0])
-        for t in ORDER[2:]:
-            look_up(t)
+        for t in ORDER[1:]:
             compare(t)
-        for t in ORDER[2:]:
-            smaller_on_vector(t)
         for t in ORDER[1:]:
             choose(t)
 

@@ -1,6 +1,7 @@
 from contextlib import ExitStack
 
 import concourse.mybir as mybir
+from concourse.masks import make_identity
 
 K, T, N, U = 512, 1024, 512, 2048
 FLOPS = 2 * K * N * T
@@ -19,10 +20,14 @@ ACT = mybir.ActivationFunctionType
 P = 128
 PACK = 4
 BANK = 512
+HALVES = T // BANK
 GROUP = 512
-ORDER = (0, 2, 1, 3)
-POOL_SHARE = (0,256,704,896)
-POOL_ROUNDS = 640
+ON_VECTOR = (0, 1)
+ON_POOL = (2, 3)
+QUARTER = BANK // 2
+W_ON_SCALAR = 60
+PIECES = ((2, QUARTER, QUARTER), (2, BANK, BANK), (3, 0, BANK), (3, BANK, BANK))
+POOL_ROUNDS = 1536
 
 CHUNKS = [(0, 256, True), (256, 256, True), (512, 256, False), (768, 256, False), (1024, 128, True),
           (1152, 256, True), (1408, 128, False), (1536, 256, False), (1792, 256, False)]
@@ -47,108 +52,125 @@ def tile_picked_widxput_min_lo_kernel(tc, x_words, x_scales, mem, w1, slot, out_
         x_codes = keep.tile([P, 2 * T], U8, name="x_codes", align_bytes=64)
         nc.vector.memset(x_plane[:].bitcast(I32), 0)
         nc.sync.dma_start(offsets[:], slot)
-        for t in ORDER[:2]:
+        for t in range(2):
             nc.sync.dma_start(store[t][:], mem_rows[:, t, :])
         for q in range(4):
             nc.sync.dma_start(x_plane[32 * q : 32 * q + 4, :].bitcast(I32), x_scales[0, 4 * q : 4 * q + 4, :].bitcast(I32))
-        for t in ORDER[2:]:
+        for t in range(2, PACK):
             nc.sync.dma_start(store[t][:], mem_rows[:, t, :])
         nc.sync.dma_start(w_raw[:], w1.rearrange("(p j) c -> p j c", j=PACK))
         nc.sync.dma_start(x_codes[:].bitcast(I32), x_words[0].bitcast(I32))
 
-        w_by_t = w_raw[:].rearrange("p j (m t) -> p t m j", t=PACK)
-        w_round = [keep.tile([P, P, PACK], BF16, name="w_round%d" % t, align_bytes=64) for t in range(PACK)]
-        w_codes = keep.tile([P, N], U32, name="w_codes", align_bytes=64)
-        w_plane = keep.tile([P, N], U8, name="w_plane", align_bytes=64)
-        banks = [[psum.tile([P, BANK], F32, name="bank%d_%d" % (t, h)) for h in range(T // BANK)] for t in range(PACK)]
+        ident_f32 = keep.tile([P, P], F32, name="ident_f32")
+        ident_bf16 = keep.tile([P, P], BF16, name="ident_bf16")
+        make_identity(nc, ident_f32[:])
+        make_identity(nc, ident_bf16[:])
 
-        def project(t):
-            cols = slice(P * t, P * (t + 1))
-            nc.vector.quantize_mx(out=w_codes[:, cols].bitcast(FP8X4), scales=w_plane[:, cols], in_=w_round[t][:].rearrange("p m j -> p (m j)"))
-            for h in range(T // BANK):
-                nc.tensor.matmul_mx(
-                    out=banks[t][h][:],
-                    lhsT=w_codes[:, cols].bitcast(FP8X4),
-                    lhsT_scale=w_plane[:, cols],
-                    rhs=x_codes[:, 2 * BANK * h : 2 * BANK * (h + 1)].bitcast(FP4X4),
-                    rhs_scale=x_plane[:, BANK * h : BANK * (h + 1)],
-                    start=True,
-                    stop=True,
-                )
+        old_pair = keep.tile([P, 2, T], F32, name="old_pair")
+        new_pair = keep.tile([P, 2, T], F32, name="new_pair")
+        old = [old_pair[:, t, :] if t in ON_VECTOR else keep.tile([P, T], F32, name="old%d" % t)[:] for t in range(PACK)]
+        new = [new_pair[:, t, :] if t in ON_VECTOR else keep.tile([P, T], F32, name="new%d" % t)[:] for t in range(PACK)]
+        for t in range(PACK):
+            nc.vector.tensor_copy(old[t], store[t][:].indirect(offsets[:]))
 
+        w_by_m = w_raw[:].rearrange("p j (m t) -> p m t j", t=PACK)
+        w_round = keep.tile([P, PACK, P, PACK], BF16, name="w_round", align_bytes=64)
+        w_round_by_m = w_round[:].rearrange("p t m j -> p m t j")
+        w_codes = [keep.tile([P, P], U32, name="w_codes%d" % t, align_bytes=64) for t in range(PACK)]
+        w_plane = [keep.tile([P, P], U8, name="w_plane%d" % t, align_bytes=64) for t in range(PACK)]
+        nc.scalar.copy(w_round_by_m[:, :W_ON_SCALAR], w_by_m[:, :W_ON_SCALAR])
+        nc.vector.tensor_copy(w_round_by_m[:, W_ON_SCALAR:], w_by_m[:, W_ON_SCALAR:])
+        for t in range(PACK):
+            nc.vector.quantize_mx(out=w_codes[t][:].bitcast(FP8X4), scales=w_plane[t][:], in_=w_round[:, t].rearrange("p m j -> p (m j)"))
+
+        def project(out, t, first, width):
+            nc.tensor.matmul_mx(
+                out=out,
+                lhsT=w_codes[t][:].bitcast(FP8X4),
+                lhsT_scale=w_plane[t][:],
+                rhs=x_codes[:, 2 * first : 2 * (first + width)].bitcast(FP4X4),
+                rhs_scale=x_plane[:, first : first + width],
+                start=True,
+                stop=True,
+            )
+
+        for b in range(T // QUARTER):
+            cols = slice(QUARTER * b, QUARTER * (b + 1))
+            y_pair = psum.tile([P, 2, QUARTER], F32, name="bank%d" % b)
+            for t in ON_VECTOR:
+                project(y_pair[:, t, :], t, QUARTER * b, QUARTER)
+            nc.vector.tensor_tensor(new_pair[:, :, cols], old_pair[:, :, cols], y_pair[:], ALU.min)
+
+        minus_y = {t: keep.tile([P, T], F32, name="minus_y%d" % t) for t in ON_POOL}
+        keep_old = {t: keep.tile([P, T], F32, name="keep_old%d" % t) for t in ON_POOL}
+        take_new = {t: keep.tile([P, T], F32, name="take_new%d" % t) for t in ON_POOL}
         signs = shared.tile([P, U * PACK], BF16, name="signs", align_bytes=64, offset=0)
-        share = dict(zip(ORDER, POOL_SHARE))
-        old = [keep.tile([P, T], F32, name="old%d" % t) for t in range(PACK)]
-        new = [keep.tile([P, T], F32, name="new%d" % t) for t in range(PACK)]
-        y = {t: keep.tile([P, share[t]], F32, name="y%d" % t) for t in ORDER[1:]}
-        keep_old = {t: keep.tile([P, share[t]], F32, name="keep_old%d" % t) for t in ORDER[1:]}
-        take_new = {t: keep.tile([P, share[t]], F32, name="take_new%d" % t) for t in ORDER[1:]}
+        plus_half, minus_half = signs[:, BANK : BANK + 1], signs[:, BANK + 2 : BANK + 3]
+        nc.vector.memset(plus_half, 0.5)
+        nc.vector.memset(minus_half, -0.5)
 
-        def bank_pieces(first, end):
-            return [(h, max(first, BANK * h), min(end, BANK * (h + 1))) for h in range(T // BANK) if max(first, BANK * h) < min(end, BANK * (h + 1))]
+        def fetch_y(i):
+            t, first, width = PIECES[i]
+            y = psum.tile([P, width], F32, name="bank%d" % (4 + i))
+            project(y[:], t, first, width)
+            nc.scalar.activation(minus_y[t][:, first : first + width], y[:], ACT.Copy, scale=-1.0)
 
-        def look_up(t):
-            nc.vector.tensor_copy(old[t][:], store[t][:].indirect(offsets[:]))
+        def make_masks(i):
+            t, first, width = PIECES[i]
+            cols = slice(first, first + width)
+            gap = psum.tile([P, width], F32, name="bank%d" % (4 + i))
+            for b in range(width // P):
+                block = slice(first + P * b, first + P * (b + 1))
+                nc.tensor.matmul(gap[:, P * b : P * (b + 1)], old[t][:, block], ident_f32[:], start=True, stop=False, is_transpose=True)
+                nc.tensor.matmul(gap[:, P * b : P * (b + 1)], minus_y[t][:, block], ident_f32[:], start=False, stop=True, is_transpose=True)
+            turned = signs[:, U * i : U * i + width]
+            nc.scalar.activation(turned, gap[:], ACT.Sign)
+            side = psum.tile([P, width], BF16, name="bank%d" % (4 + i))
+            for b in range(width // P):
+                nc.tensor.transpose(side[:, P * b : P * (b + 1)], turned[:, P * b : P * (b + 1)], ident_bf16[:])
+            nc.scalar.activation(keep_old[t][:, cols], side[:], ACT.Identity, scale=-0.5, bias=plus_half)
+            nc.scalar.activation(take_new[t][:, cols], side[:], ACT.Identity, scale=-0.5, bias=minus_half)
 
-        def smaller_on_vector(t):
-            for h, a, b in bank_pieces(0, T - share[t]):
-                nc.vector.tensor_tensor(new[t][:, a:b], old[t][:, a:b], banks[t][h][:, a - BANK * h : b - BANK * h], ALU.min)
+        fetch_y(0)
+        t = ON_POOL[0]
+        y_rest = psum.tile([P, QUARTER], F32, name="bank0")
+        project(y_rest[:], t, 0, QUARTER)
+        nc.vector.tensor_tensor(new[t][:, :QUARTER], old[t][:, :QUARTER], y_rest[:], ALU.min)
 
-        def fetch_y(t):
-            first = T - share[t]
-            for h, a, b in bank_pieces(first, T):
-                nc.scalar.copy(y[t][:, a - first : b - first], banks[t][h][:, a - BANK * h : b - BANK * h])
-
-        def compare(t):
-            first = T - share[t]
-            gap = keep.tile([P, share[t]], F32, name="gap%d" % t)
-            side = signs[:, U * t : U * t + share[t]]
-            nc.gpsimd.tensor_tensor(gap[:], old[t][:, first:], y[t][:], ALU.subtract)
-            nc.scalar.activation(side, gap[:], ACT.Sign)
-            nc.scalar.activation(keep_old[t][:], side, ACT.Copy, scale=-0.5, bias=0.5)
-            nc.scalar.activation(take_new[t][:], side, ACT.Copy, scale=0.5, bias=0.5)
-
-        def choose(t):
-            first = T - share[t]
-            nc.gpsimd.tensor_tensor(keep_old[t][:], keep_old[t][:], old[t][:, first:], ALU.mult)
-            nc.gpsimd.tensor_tensor(take_new[t][:], take_new[t][:], y[t][:], ALU.mult)
-            nc.gpsimd.tensor_tensor(new[t][:, first:], keep_old[t][:], take_new[t][:], ALU.add)
+        make_masks(0)
+        for i in range(1, len(PIECES)):
+            fetch_y(i)
+        for i in range(1, len(PIECES)):
+            make_masks(i)
+        for t in ON_POOL:
+            spans = [slice(first, first + width) for tile, first, width in PIECES if tile == t]
+            for cols in spans:
+                nc.gpsimd.tensor_tensor(keep_old[t][:, cols], keep_old[t][:, cols], old[t][:, cols], ALU.mult)
+                nc.gpsimd.tensor_tensor(take_new[t][:, cols], take_new[t][:, cols], minus_y[t][:, cols], ALU.mult)
+            for cols in spans:
+                nc.gpsimd.tensor_tensor(new[t][:, cols], keep_old[t][:, cols], take_new[t][:, cols], ALU.add)
 
         rounded = [shared.tile([P, width, PACK], BF16, name="rounded%d" % c, align_bytes=64, offset=2 * PACK * first) for c, (first, width, on_vector) in enumerate(CHUNKS)]
         words = keep.tile([P, U], U32, name="words", align_bytes=64)
         plane = keep.tile([P, GROUP], U8, name="plane", align_bytes=64)
 
-        for t in ORDER:
-            look_up(t)
-        for step, t in enumerate(ORDER):
-            if step == 1:
-                nc.vector.tensor_copy(w_round[t][:], w_by_t[:, t, :, :])
-            else:
-                nc.scalar.copy(w_round[t][:], w_by_t[:, t, :, :])
-        for t in ORDER:
-            project(t)
-        for t in ORDER[1:]:
-            fetch_y(t)
-        for t in ORDER:
-            smaller_on_vector(t)
-        for t in ORDER[1:]:
-            compare(t)
-        for t in ORDER[1:]:
-            choose(t)
-
-        for t in ORDER:
-            nc.vector.tensor_copy(store[t][:].indirect(offsets[:]), new[t][:])
+        for t in range(PACK):
+            nc.vector.tensor_copy(store[t][:].indirect(offsets[:]), new[t])
             nc.sync.dma_start(out_rows[:, t, :], store[t][:])
             for c, (first, width, on_vector) in enumerate(CHUNKS):
-                if t == 3 and on_vector:
+                if t == PACK - 1 and on_vector:
                     nc.vector.tensor_copy(rounded[c][:, :, t], store[t][:, first : first + width])
             for c, (first, width, on_vector) in enumerate(CHUNKS):
                 values = store[t][:, first : first + width]
-                if t % 2 == 0:
-                    nc.scalar.copy(rounded[c][:, :, t : t + 2], values.unsqueeze(2).to_broadcast([P, width, 2]))
-                elif t == 1 and first >= U - POOL_ROUNDS:
-                    nc.gpsimd.tensor_scalar(rounded[c][:, :, t], values, 1.0, -0.0, ALU.mult, ALU.add)
-                elif not (t == 3 and on_vector):
+                if t == PACK - 2:
+                    twice = values.unsqueeze(2).to_broadcast([P, width, 2])
+                    if first < POOL_ROUNDS:
+                        nc.gpsimd.tensor_scalar(rounded[c][:, :, t:], twice, 1.0, -0.0, ALU.mult, ALU.add)
+                    else:
+                        nc.scalar.copy(rounded[c][:, :, t:], twice)
+                elif t == 1 and first < POOL_ROUNDS:
+                    nc.scalar.copy(rounded[c][:, :, t:], values.unsqueeze(2).to_broadcast([P, width, PACK - t]))
+                elif not (t == PACK - 1 and on_vector):
                     nc.scalar.copy(rounded[c][:, :, t], values)
 
         for c, (first, width, on_vector) in enumerate(CHUNKS):

@@ -24,10 +24,10 @@ HALVES = T // BANK
 GROUP = 512
 ON_VECTOR = (0, 1)
 ON_POOL = (2, 3)
-QUARTER = BANK // 2
-W_ON_SCALAR = 60
-PIECES = ((2, QUARTER, QUARTER), (2, BANK, BANK), (3, 0, BANK), (3, BANK, BANK))
-POOL_ROUNDS = 1536
+SLIVER = 64
+W_ON_SCALAR = 40
+PIECES = ((2, 0, 384), (2, 384, BANK), (3, 0, 384), (3, 384, BANK))
+POOL_ROUNDS = 1024
 
 CHUNKS = [(0, 256, True), (256, 256, True), (512, 256, False), (768, 256, False), (1024, 128, True),
           (1152, 256, True), (1408, 128, False), (1536, 256, False), (1792, 256, False)]
@@ -51,27 +51,22 @@ def tile_picked_widxput_min_lo_kernel(tc, x_words, x_scales, mem, w1, slot, out_
         x_plane = keep.tile([P, T], U8, name="x_plane", align_bytes=64)
         x_codes = keep.tile([P, 2 * T], U8, name="x_codes", align_bytes=64)
         nc.vector.memset(x_plane[:].bitcast(I32), 0)
+        nc.sync.dma_start(w_raw[:], w1.rearrange("(p j) c -> p j c", j=PACK))
         nc.sync.dma_start(offsets[:], slot)
-        for t in range(2):
-            nc.sync.dma_start(store[t][:], mem_rows[:, t, :])
+        nc.sync.dma_start(store[0][:], mem_rows[:, 0, :])
+        nc.sync.dma_start(x_codes[:].bitcast(I32), x_words[0].bitcast(I32))
         for q in range(4):
             nc.sync.dma_start(x_plane[32 * q : 32 * q + 4, :].bitcast(I32), x_scales[0, 4 * q : 4 * q + 4, :].bitcast(I32))
-        for t in range(2, PACK):
+        for t in range(1, PACK):
             nc.sync.dma_start(store[t][:], mem_rows[:, t, :])
-        nc.sync.dma_start(w_raw[:], w1.rearrange("(p j) c -> p j c", j=PACK))
-        nc.sync.dma_start(x_codes[:].bitcast(I32), x_words[0].bitcast(I32))
 
         ident_f32 = keep.tile([P, P], F32, name="ident_f32")
         ident_bf16 = keep.tile([P, P], BF16, name="ident_bf16")
         make_identity(nc, ident_f32[:])
         make_identity(nc, ident_bf16[:])
 
-        old_pair = keep.tile([P, 2, T], F32, name="old_pair")
-        new_pair = keep.tile([P, 2, T], F32, name="new_pair")
-        old = [old_pair[:, t, :] if t in ON_VECTOR else keep.tile([P, T], F32, name="old%d" % t)[:] for t in range(PACK)]
-        new = [new_pair[:, t, :] if t in ON_VECTOR else keep.tile([P, T], F32, name="new%d" % t)[:] for t in range(PACK)]
-        for t in range(PACK):
-            nc.vector.tensor_copy(old[t], store[t][:].indirect(offsets[:]))
+        old = keep.tile([P, PACK, T], F32, name="old")
+        new = keep.tile([P, PACK, T], F32, name="new")
 
         w_by_m = w_raw[:].rearrange("p j (m t) -> p m t j", t=PACK)
         w_round = keep.tile([P, PACK, P, PACK], BF16, name="w_round", align_bytes=64)
@@ -84,22 +79,36 @@ def tile_picked_widxput_min_lo_kernel(tc, x_words, x_scales, mem, w1, slot, out_
             nc.vector.quantize_mx(out=w_codes[t][:].bitcast(FP8X4), scales=w_plane[t][:], in_=w_round[:, t].rearrange("p m j -> p (m j)"))
 
         def project(out, t, first, width):
-            nc.tensor.matmul_mx(
-                out=out,
-                lhsT=w_codes[t][:].bitcast(FP8X4),
-                lhsT_scale=w_plane[t][:],
-                rhs=x_codes[:, 2 * first : 2 * (first + width)].bitcast(FP4X4),
-                rhs_scale=x_plane[:, first : first + width],
-                start=True,
-                stop=True,
-            )
+            done = 0
+            for count in (BANK, BANK // 2, BANK // 4, BANK // 8):
+                if width - done >= count:
+                    start = first + done
+                    nc.tensor.matmul_mx(
+                        out=out[:, done : done + count],
+                        lhsT=w_codes[t][:].bitcast(FP8X4),
+                        lhsT_scale=w_plane[t][:],
+                        rhs=x_codes[:, 2 * start : 2 * (start + count)].bitcast(FP4X4),
+                        rhs_scale=x_plane[:, start : start + count],
+                        start=True,
+                        stop=True,
+                    )
+                    done = done + count
 
-        for b in range(T // QUARTER):
-            cols = slice(QUARTER * b, QUARTER * (b + 1))
-            y_pair = psum.tile([P, 2, QUARTER], F32, name="bank%d" % b)
-            for t in ON_VECTOR:
-                project(y_pair[:, t, :], t, QUARTER * b, QUARTER)
-            nc.vector.tensor_tensor(new_pair[:, :, cols], old_pair[:, :, cols], y_pair[:], ALU.min)
+        def smaller_on_vector(bank, tiles, first, width):
+            y = psum.tile([P, len(tiles), width], F32, name="bank%d" % bank)
+            for i, t in enumerate(tiles):
+                project(y[:, i, :], t, first, width)
+            rows, cols = slice(tiles[0], tiles[-1] + 1), slice(first, first + width)
+            nc.vector.tensor_tensor(new[:, rows, cols], old[:, rows, cols], y[:], ALU.min)
+
+        def look_up(t, halves):
+            for h in halves:
+                nc.vector.tensor_copy(old[:, t, BANK * h : BANK * (h + 1)], store[t][:].indirect(offsets[:, BANK // 16 * h : BANK // 16 * (h + 1)]))
+
+        for t in ON_VECTOR:
+            look_up(t, (0, 1))
+            smaller_on_vector(2 * t, [t], 0, BANK)
+            smaller_on_vector(2 * t + 1, [t], BANK, T - SLIVER - BANK)
 
         minus_y = {t: keep.tile([P, T], F32, name="minus_y%d" % t) for t in ON_POOL}
         keep_old = {t: keep.tile([P, T], F32, name="keep_old%d" % t) for t in ON_POOL}
@@ -121,7 +130,7 @@ def tile_picked_widxput_min_lo_kernel(tc, x_words, x_scales, mem, w1, slot, out_
             gap = psum.tile([P, width], F32, name="bank%d" % (4 + i))
             for b in range(width // P):
                 block = slice(first + P * b, first + P * (b + 1))
-                nc.tensor.matmul(gap[:, P * b : P * (b + 1)], old[t][:, block], ident_f32[:], start=True, stop=False, is_transpose=True)
+                nc.tensor.matmul(gap[:, P * b : P * (b + 1)], old[:, t, block], ident_f32[:], start=True, stop=False, is_transpose=True)
                 nc.tensor.matmul(gap[:, P * b : P * (b + 1)], minus_y[t][:, block], ident_f32[:], start=False, stop=True, is_transpose=True)
             turned = signs[:, U * i : U * i + width]
             nc.scalar.activation(turned, gap[:], ACT.Sign)
@@ -131,31 +140,28 @@ def tile_picked_widxput_min_lo_kernel(tc, x_words, x_scales, mem, w1, slot, out_
             nc.scalar.activation(keep_old[t][:, cols], side[:], ACT.Identity, scale=-0.5, bias=plus_half)
             nc.scalar.activation(take_new[t][:, cols], side[:], ACT.Identity, scale=-0.5, bias=minus_half)
 
-        fetch_y(0)
-        t = ON_POOL[0]
-        y_rest = psum.tile([P, QUARTER], F32, name="bank0")
-        project(y_rest[:], t, 0, QUARTER)
-        nc.vector.tensor_tensor(new[t][:, :QUARTER], old[t][:, :QUARTER], y_rest[:], ALU.min)
-
-        make_masks(0)
-        for i in range(1, len(PIECES)):
+        for i in range(len(PIECES)):
             fetch_y(i)
-        for i in range(1, len(PIECES)):
+        nc.vector.tensor_copy(old[:, 2, :], store[2][:].indirect(offsets[:]))
+        look_up(3, (1, 0))
+        smaller_on_vector(0, list(range(PACK)), T - SLIVER, SLIVER)
+        smaller_on_vector(1, ON_POOL, T - 2 * SLIVER, SLIVER)
+        for i in range(len(PIECES)):
             make_masks(i)
         for t in ON_POOL:
             spans = [slice(first, first + width) for tile, first, width in PIECES if tile == t]
             for cols in spans:
-                nc.gpsimd.tensor_tensor(keep_old[t][:, cols], keep_old[t][:, cols], old[t][:, cols], ALU.mult)
+                nc.gpsimd.tensor_tensor(keep_old[t][:, cols], keep_old[t][:, cols], old[:, t, cols], ALU.mult)
                 nc.gpsimd.tensor_tensor(take_new[t][:, cols], take_new[t][:, cols], minus_y[t][:, cols], ALU.mult)
             for cols in spans:
-                nc.gpsimd.tensor_tensor(new[t][:, cols], keep_old[t][:, cols], take_new[t][:, cols], ALU.add)
+                nc.gpsimd.tensor_tensor(new[:, t, cols], keep_old[t][:, cols], take_new[t][:, cols], ALU.add)
 
         rounded = [shared.tile([P, width, PACK], BF16, name="rounded%d" % c, align_bytes=64, offset=2 * PACK * first) for c, (first, width, on_vector) in enumerate(CHUNKS)]
         words = keep.tile([P, U], U32, name="words", align_bytes=64)
         plane = keep.tile([P, GROUP], U8, name="plane", align_bytes=64)
 
         for t in range(PACK):
-            nc.vector.tensor_copy(store[t][:].indirect(offsets[:]), new[t])
+            nc.vector.tensor_copy(store[t][:].indirect(offsets[:]), new[:, t, :])
             nc.sync.dma_start(out_rows[:, t, :], store[t][:])
             for c, (first, width, on_vector) in enumerate(CHUNKS):
                 if t == PACK - 1 and on_vector:

@@ -20,14 +20,18 @@ ACT = mybir.ActivationFunctionType
 P = 128
 PACK = 4
 BANK = 512
-HALVES = T // BANK
+LANES = 16
+QUADRANTS = 4
 GROUP = 512
-ON_VECTOR = (0, 1)
-ON_POOL = (2, 3)
+
+ORDER = (0, 2, 3, 1)
+VECTOR_STEPS = (0, 1)
+MASKED_STEPS = (2, 3)
 SLIVER = 64
+MASKED = T - 2 * SLIVER
+PIECES = tuple((step, first, width) for step in MASKED_STEPS for first, width in ((0, MASKED - BANK), (MASKED - BANK, BANK)))
 W_ON_SCALAR = 40
-PIECES = ((2, 0, 384), (2, 384, BANK), (3, 0, 384), (3, 384, BANK))
-POOL_ROUNDS = 1024
+POOL_FROM = 1536
 
 CHUNKS = [(0, 256, True), (256, 256, True), (512, 256, False), (768, 256, False), (1024, 128, True),
           (1152, 256, True), (1408, 128, False), (1536, 256, False), (1792, 256, False)]
@@ -45,20 +49,20 @@ def tile_picked_widxput_min_lo_kernel(tc, x_words, x_scales, mem, w1, slot, out_
         shared = ctx.enter_context(tc.tile_pool(name="shared", bufs=1))
         psum = ctx.enter_context(tc.psum_pool(name="psum", bufs=1))
 
-        offsets = keep.tile([P, T // 16], U16, name="offsets")
-        store = [keep.tile([P, U], F32, name="store%d" % t) for t in range(PACK)]
+        offsets = keep.tile([P, T // LANES], U16, name="offsets")
+        store = [keep.tile([P, U], F32, name="store%d" % step) for step in range(PACK)]
         w_raw = keep.tile([P, PACK, N], F32, name="w_raw")
         x_plane = keep.tile([P, T], U8, name="x_plane", align_bytes=64)
         x_codes = keep.tile([P, 2 * T], U8, name="x_codes", align_bytes=64)
         nc.vector.memset(x_plane[:].bitcast(I32), 0)
         nc.sync.dma_start(w_raw[:], w1.rearrange("(p j) c -> p j c", j=PACK))
         nc.sync.dma_start(offsets[:], slot)
-        nc.sync.dma_start(store[0][:], mem_rows[:, 0, :])
+        nc.sync.dma_start(store[0][:], mem_rows[:, ORDER[0], :])
         nc.sync.dma_start(x_codes[:].bitcast(I32), x_words[0].bitcast(I32))
-        for q in range(4):
+        for q in range(QUADRANTS):
             nc.sync.dma_start(x_plane[32 * q : 32 * q + 4, :].bitcast(I32), x_scales[0, 4 * q : 4 * q + 4, :].bitcast(I32))
-        for t in range(1, PACK):
-            nc.sync.dma_start(store[t][:], mem_rows[:, t, :])
+        for step in range(1, PACK):
+            nc.sync.dma_start(store[step][:], mem_rows[:, ORDER[step], :])
 
         ident_f32 = keep.tile([P, P], F32, name="ident_f32")
         ident_bf16 = keep.tile([P, P], BF16, name="ident_bf16")
@@ -71,22 +75,22 @@ def tile_picked_widxput_min_lo_kernel(tc, x_words, x_scales, mem, w1, slot, out_
         w_by_m = w_raw[:].rearrange("p j (m t) -> p m t j", t=PACK)
         w_round = keep.tile([P, PACK, P, PACK], BF16, name="w_round", align_bytes=64)
         w_round_by_m = w_round[:].rearrange("p t m j -> p m t j")
-        w_codes = [keep.tile([P, P], U32, name="w_codes%d" % t, align_bytes=64) for t in range(PACK)]
-        w_plane = [keep.tile([P, P], U8, name="w_plane%d" % t, align_bytes=64) for t in range(PACK)]
+        w_codes = [keep.tile([P, P], U32, name="w_codes%d" % step, align_bytes=64) for step in range(PACK)]
+        w_plane = [keep.tile([P, P], U8, name="w_plane%d" % step, align_bytes=64) for step in range(PACK)]
         nc.scalar.copy(w_round_by_m[:, :W_ON_SCALAR], w_by_m[:, :W_ON_SCALAR])
         nc.vector.tensor_copy(w_round_by_m[:, W_ON_SCALAR:], w_by_m[:, W_ON_SCALAR:])
-        for t in range(PACK):
-            nc.vector.quantize_mx(out=w_codes[t][:].bitcast(FP8X4), scales=w_plane[t][:], in_=w_round[:, t].rearrange("p m j -> p (m j)"))
+        for step, t in enumerate(ORDER):
+            nc.vector.quantize_mx(out=w_codes[step][:].bitcast(FP8X4), scales=w_plane[step][:], in_=w_round[:, t].rearrange("p m j -> p (m j)"))
 
-        def project(out, t, first, width):
+        def project(out, step, first, width):
             done = 0
             for count in (BANK, BANK // 2, BANK // 4, BANK // 8):
                 if width - done >= count:
                     start = first + done
                     nc.tensor.matmul_mx(
                         out=out[:, done : done + count],
-                        lhsT=w_codes[t][:].bitcast(FP8X4),
-                        lhsT_scale=w_plane[t][:],
+                        lhsT=w_codes[step][:].bitcast(FP8X4),
+                        lhsT_scale=w_plane[step][:],
                         rhs=x_codes[:, 2 * start : 2 * (start + count)].bitcast(FP4X4),
                         rhs_scale=x_plane[:, start : start + count],
                         start=True,
@@ -94,89 +98,84 @@ def tile_picked_widxput_min_lo_kernel(tc, x_words, x_scales, mem, w1, slot, out_
                     )
                     done = done + count
 
-        def smaller_on_vector(bank, tiles, first, width):
-            y = psum.tile([P, len(tiles), width], F32, name="bank%d" % bank)
-            for i, t in enumerate(tiles):
-                project(y[:, i, :], t, first, width)
-            rows, cols = slice(tiles[0], tiles[-1] + 1), slice(first, first + width)
+        def smaller_on_vector(bank, steps, first, width):
+            y = psum.tile([P, len(steps), width], F32, name="bank%d" % bank)
+            for i, step in enumerate(steps):
+                project(y[:, i, :], step, first, width)
+            rows, cols = slice(steps[0], steps[-1] + 1), slice(first, first + width)
             nc.vector.tensor_tensor(new[:, rows, cols], old[:, rows, cols], y[:], ALU.min)
 
-        def look_up(t, halves):
+        def look_up(step, halves):
             for h in halves:
-                nc.vector.tensor_copy(old[:, t, BANK * h : BANK * (h + 1)], store[t][:].indirect(offsets[:, BANK // 16 * h : BANK // 16 * (h + 1)]))
+                nc.vector.tensor_copy(old[:, step, BANK * h : BANK * (h + 1)], store[step][:].indirect(offsets[:, BANK // LANES * h : BANK // LANES * (h + 1)]))
 
-        for t in ON_VECTOR:
-            look_up(t, (0, 1))
-            smaller_on_vector(2 * t, [t], 0, BANK)
-            smaller_on_vector(2 * t + 1, [t], BANK, T - SLIVER - BANK)
+        for step in VECTOR_STEPS:
+            look_up(step, (0, 1))
+            smaller_on_vector(2 * step, [step], 0, BANK)
+            smaller_on_vector(2 * step + 1, [step], BANK, T - SLIVER - BANK)
 
-        minus_y = {t: keep.tile([P, T], F32, name="minus_y%d" % t) for t in ON_POOL}
-        keep_old = {t: keep.tile([P, T], F32, name="keep_old%d" % t) for t in ON_POOL}
-        take_new = {t: keep.tile([P, T], F32, name="take_new%d" % t) for t in ON_POOL}
+        minus_y = {step: keep.tile([P, MASKED], F32, name="minus_y%d" % step) for step in MASKED_STEPS}
+        keep_old = {step: keep.tile([P, MASKED], F32, name="keep_old%d" % step) for step in MASKED_STEPS}
+        take_new = {step: keep.tile([P, MASKED], F32, name="take_new%d" % step) for step in MASKED_STEPS}
         signs = shared.tile([P, U * PACK], BF16, name="signs", align_bytes=64, offset=0)
-        plus_half, minus_half = signs[:, BANK : BANK + 1], signs[:, BANK + 2 : BANK + 3]
-        nc.vector.memset(plus_half, 0.5)
+        minus_half = signs[:, BANK : BANK + 1]
         nc.vector.memset(minus_half, -0.5)
+        first_piece_bank = 2 * len(VECTOR_STEPS)
 
         def fetch_y(i):
-            t, first, width = PIECES[i]
-            y = psum.tile([P, width], F32, name="bank%d" % (4 + i))
-            project(y[:], t, first, width)
-            nc.scalar.activation(minus_y[t][:, first : first + width], y[:], ACT.Copy, scale=-1.0)
+            step, first, width = PIECES[i]
+            y = psum.tile([P, width], F32, name="bank%d" % (first_piece_bank + i))
+            project(y[:], step, first, width)
+            nc.scalar.activation(minus_y[step][:, first : first + width], y[:], ACT.Copy, scale=-1.0)
 
         def make_masks(i):
-            t, first, width = PIECES[i]
+            step, first, width = PIECES[i]
             cols = slice(first, first + width)
-            gap = psum.tile([P, width], F32, name="bank%d" % (4 + i))
+            gap = psum.tile([P, width], F32, name="bank%d" % (first_piece_bank + i))
             for b in range(width // P):
                 block = slice(first + P * b, first + P * (b + 1))
-                nc.tensor.matmul(gap[:, P * b : P * (b + 1)], old[:, t, block], ident_f32[:], start=True, stop=False, is_transpose=True)
-                nc.tensor.matmul(gap[:, P * b : P * (b + 1)], minus_y[t][:, block], ident_f32[:], start=False, stop=True, is_transpose=True)
+                nc.tensor.matmul(gap[:, P * b : P * (b + 1)], old[:, step, block], ident_f32[:], start=True, stop=False, is_transpose=True)
+                nc.tensor.matmul(gap[:, P * b : P * (b + 1)], minus_y[step][:, block], ident_f32[:], start=False, stop=True, is_transpose=True)
             turned = signs[:, U * i : U * i + width]
             nc.scalar.activation(turned, gap[:], ACT.Sign)
-            side = psum.tile([P, width], BF16, name="bank%d" % (4 + i))
+            side = psum.tile([P, width], BF16, name="bank%d" % (first_piece_bank + i))
             for b in range(width // P):
                 nc.tensor.transpose(side[:, P * b : P * (b + 1)], turned[:, P * b : P * (b + 1)], ident_bf16[:])
-            nc.scalar.activation(keep_old[t][:, cols], side[:], ACT.Identity, scale=-0.5, bias=plus_half)
-            nc.scalar.activation(take_new[t][:, cols], side[:], ACT.Identity, scale=-0.5, bias=minus_half)
+            nc.scalar.activation(keep_old[step][:, cols], side[:], ACT.Copy, scale=-0.5, bias=0.5)
+            nc.scalar.activation(take_new[step][:, cols], side[:], ACT.Identity, scale=-0.5, bias=minus_half)
 
         for i in range(len(PIECES)):
             fetch_y(i)
         nc.vector.tensor_copy(old[:, 2, :], store[2][:].indirect(offsets[:]))
         look_up(3, (1, 0))
-        smaller_on_vector(0, list(range(PACK)), T - SLIVER, SLIVER)
-        smaller_on_vector(1, ON_POOL, T - 2 * SLIVER, SLIVER)
+        smaller_on_vector(0, range(PACK), T - SLIVER, SLIVER)
+        smaller_on_vector(1, MASKED_STEPS, MASKED, SLIVER)
         for i in range(len(PIECES)):
             make_masks(i)
-        for t in ON_POOL:
-            spans = [slice(first, first + width) for tile, first, width in PIECES if tile == t]
-            for cols in spans:
-                nc.gpsimd.tensor_tensor(keep_old[t][:, cols], keep_old[t][:, cols], old[:, t, cols], ALU.mult)
-                nc.gpsimd.tensor_tensor(take_new[t][:, cols], take_new[t][:, cols], minus_y[t][:, cols], ALU.mult)
-            for cols in spans:
-                nc.gpsimd.tensor_tensor(new[:, t, cols], keep_old[t][:, cols], take_new[t][:, cols], ALU.add)
+        for step in MASKED_STEPS:
+            nc.gpsimd.tensor_tensor(keep_old[step][:], keep_old[step][:], old[:, step, :MASKED], ALU.mult)
+            nc.gpsimd.tensor_tensor(take_new[step][:], take_new[step][:], minus_y[step][:], ALU.mult)
+            nc.gpsimd.tensor_tensor(new[:, step, :MASKED], keep_old[step][:], take_new[step][:], ALU.add)
 
         rounded = [shared.tile([P, width, PACK], BF16, name="rounded%d" % c, align_bytes=64, offset=2 * PACK * first) for c, (first, width, on_vector) in enumerate(CHUNKS)]
         words = keep.tile([P, U], U32, name="words", align_bytes=64)
         plane = keep.tile([P, GROUP], U8, name="plane", align_bytes=64)
 
-        for t in range(PACK):
-            nc.vector.tensor_copy(store[t][:].indirect(offsets[:]), new[:, t, :])
-            nc.sync.dma_start(out_rows[:, t, :], store[t][:])
+        for step, t in enumerate(ORDER):
+            nc.vector.tensor_copy(store[step][:].indirect(offsets[:]), new[:, step, :])
+            nc.sync.dma_start(out_rows[:, t, :], store[step][:])
+            last = step == PACK - 1
             for c, (first, width, on_vector) in enumerate(CHUNKS):
-                if t == PACK - 1 and on_vector:
-                    nc.vector.tensor_copy(rounded[c][:, :, t], store[t][:, first : first + width])
+                if last and on_vector:
+                    nc.vector.tensor_copy(rounded[c][:, :, t], store[step][:, first : first + width])
             for c, (first, width, on_vector) in enumerate(CHUNKS):
-                values = store[t][:, first : first + width]
-                if t == PACK - 2:
-                    twice = values.unsqueeze(2).to_broadcast([P, width, 2])
-                    if first < POOL_ROUNDS:
-                        nc.gpsimd.tensor_scalar(rounded[c][:, :, t:], twice, 1.0, -0.0, ALU.mult, ALU.add)
-                    else:
-                        nc.scalar.copy(rounded[c][:, :, t:], twice)
-                elif t == 1 and first < POOL_ROUNDS:
-                    nc.scalar.copy(rounded[c][:, :, t:], values.unsqueeze(2).to_broadcast([P, width, PACK - t]))
-                elif not (t == PACK - 1 and on_vector):
+                values = store[step][:, first : first + width]
+                on_pool = first >= POOL_FROM
+                if (step == 0 and on_vector) or (step == 1 and on_pool):
+                    nc.scalar.copy(rounded[c][:, :, t : t + 2], values.unsqueeze(2).to_broadcast([P, width, 2]))
+                elif step == 2 and on_pool:
+                    nc.gpsimd.tensor_scalar(rounded[c][:, :, t], values, 1.0, -0.0, ALU.mult, ALU.add)
+                elif not (last and on_vector):
                     nc.scalar.copy(rounded[c][:, :, t], values)
 
         for c, (first, width, on_vector) in enumerate(CHUNKS):
@@ -188,7 +187,7 @@ def tile_picked_widxput_min_lo_kernel(tc, x_words, x_scales, mem, w1, slot, out_
             )
         for first, width in WORD_STORES:
             nc.sync.dma_start(out_words[:, first : first + width], words[:, first : first + width].bitcast(I32))
-        for q in range(4):
+        for q in range(QUADRANTS):
             nc.scalar.dma_start(
                 out_2[0, 4 * q : 4 * q + 4, :].bitcast(I32).rearrange("r (g c) -> g r c", g=U // GROUP),
                 plane[32 * q : 32 * q + 4 * (U // GROUP), :].bitcast(I32),

@@ -24,18 +24,18 @@ LANES = 16
 QUADRANTS = 4
 GROUP = 512
 
-ORDER = (0, 2, 3, 1)
-VECTOR_STEPS = (0, 1)
-MASKED_STEPS = (2, 3)
-SLIVER = 64
-MASKED = T - 2 * SLIVER
-PIECES = tuple((step, first, width) for step in MASKED_STEPS for first, width in ((0, MASKED - BANK), (MASKED - BANK, BANK)))
-W_ON_SCALAR = 40
+ORDER = (0, 1, 2, 3)
+VECTOR_STEPS = (0,)
+MASKED_STEPS = (1, 2, 3)
+SLIVER = 128
+MASKED = {1: T - 2 * SLIVER, 2: T - SLIVER, 3: T - SLIVER}
+PIECES = tuple((step, first, width) for step in MASKED_STEPS for first, width in ((0, MASKED[step] - BANK), (MASKED[step] - BANK, BANK)))
+W_ON_SCALAR = 80
 POOL_FROM = 1536
 
-CHUNKS = [(0, 256, True), (256, 256, True), (512, 256, False), (768, 256, False), (1024, 128, True),
-          (1152, 256, True), (1408, 128, False), (1536, 256, False), (1792, 256, False)]
-WORD_STORES = [(0, 768), (768, 640), (1408, 384), (1792, 256)]
+CHUNKS = [(0, 512, True), (512, 384, True), (896, 384, False), (1280, 256, False), (1536, 256, False), (1792, 256, False)]
+CALLS = [(0, 256), (256, 256), (512, 256), (768, 128), (896, 128), (1024, 256), (1280, 256), (1536, 256), (1792, 256)]
+WORD_STORES = [(0, 768), (768, 512), (1280, 512), (1792, 256)]
 
 
 def tile_picked_widxput_min_lo_kernel(tc, x_words, x_scales, mem, w1, slot, out_0, out_1, out_2):
@@ -55,13 +55,14 @@ def tile_picked_widxput_min_lo_kernel(tc, x_words, x_scales, mem, w1, slot, out_
         x_plane = keep.tile([P, T], U8, name="x_plane", align_bytes=64)
         x_codes = keep.tile([P, 2 * T], U8, name="x_codes", align_bytes=64)
         nc.vector.memset(x_plane[:].bitcast(I32), 0)
-        nc.sync.dma_start(w_raw[:], w1.rearrange("(p j) c -> p j c", j=PACK))
         nc.sync.dma_start(offsets[:], slot)
         nc.sync.dma_start(store[0][:], mem_rows[:, ORDER[0], :])
+        nc.sync.dma_start(w_raw[:], w1.rearrange("(p j) c -> p j c", j=PACK))
+        nc.sync.dma_start(store[1][:], mem_rows[:, ORDER[1], :])
         nc.sync.dma_start(x_codes[:].bitcast(I32), x_words[0].bitcast(I32))
         for q in range(QUADRANTS):
             nc.sync.dma_start(x_plane[32 * q : 32 * q + 4, :].bitcast(I32), x_scales[0, 4 * q : 4 * q + 4, :].bitcast(I32))
-        for step in range(1, PACK):
+        for step in range(2, PACK):
             nc.sync.dma_start(store[step][:], mem_rows[:, ORDER[step], :])
 
         ident_f32 = keep.tile([P, P], F32, name="ident_f32")
@@ -69,18 +70,21 @@ def tile_picked_widxput_min_lo_kernel(tc, x_words, x_scales, mem, w1, slot, out_
         make_identity(nc, ident_f32[:])
         make_identity(nc, ident_bf16[:])
 
-        old = keep.tile([P, PACK, T], F32, name="old")
+        old = keep.tile([P, 2 * PACK, T], F32, name="old", align_bytes=64)
         new = keep.tile([P, PACK, T], F32, name="new")
 
+        nc.vector.tensor_copy(old[:, 0, :], store[0][:].indirect(offsets[:]))
+
         w_by_m = w_raw[:].rearrange("p j (m t) -> p m t j", t=PACK)
-        w_round = keep.tile([P, PACK, P, PACK], BF16, name="w_round", align_bytes=64)
-        w_round_by_m = w_round[:].rearrange("p t m j -> p m t j")
+        w_round = [old[:, 1, BANK * h : BANK * (h + 1)].bitcast(BF16).rearrange("p (t m j) -> p t m j", t=2, j=PACK) for h in range(2)]
+        w_round_by_m = [half.rearrange("p t m j -> p m t j") for half in w_round]
         w_codes = [keep.tile([P, P], U32, name="w_codes%d" % step, align_bytes=64) for step in range(PACK)]
         w_plane = [keep.tile([P, P], U8, name="w_plane%d" % step, align_bytes=64) for step in range(PACK)]
-        nc.scalar.copy(w_round_by_m[:, :W_ON_SCALAR], w_by_m[:, :W_ON_SCALAR])
-        nc.vector.tensor_copy(w_round_by_m[:, W_ON_SCALAR:], w_by_m[:, W_ON_SCALAR:])
+        nc.vector.tensor_copy(w_round_by_m[0], w_by_m[:, :, :2])
+        nc.scalar.copy(w_round_by_m[1][:, :W_ON_SCALAR], w_by_m[:, :W_ON_SCALAR, 2:])
+        nc.vector.tensor_copy(w_round_by_m[1][:, W_ON_SCALAR:], w_by_m[:, W_ON_SCALAR:, 2:])
         for step, t in enumerate(ORDER):
-            nc.vector.quantize_mx(out=w_codes[step][:].bitcast(FP8X4), scales=w_plane[step][:], in_=w_round[:, t].rearrange("p m j -> p (m j)"))
+            nc.vector.quantize_mx(out=w_codes[step][:].bitcast(FP8X4), scales=w_plane[step][:], in_=w_round[t // 2][:, t % 2].rearrange("p m j -> p (m j)"))
 
         def project(out, step, first, width):
             done = 0
@@ -105,20 +109,25 @@ def tile_picked_widxput_min_lo_kernel(tc, x_words, x_scales, mem, w1, slot, out_
             rows, cols = slice(steps[0], steps[-1] + 1), slice(first, first + width)
             nc.vector.tensor_tensor(new[:, rows, cols], old[:, rows, cols], y[:], ALU.min)
 
-        def look_up(step, halves):
-            for h in halves:
-                nc.vector.tensor_copy(old[:, step, BANK * h : BANK * (h + 1)], store[step][:].indirect(offsets[:, BANK // LANES * h : BANK // LANES * (h + 1)]))
+        def look_up(step, first, width):
+            nc.vector.tensor_copy(old[:, step, first : first + width], store[step][:].indirect(offsets[:, first // LANES : (first + width) // LANES]))
 
-        for step in VECTOR_STEPS:
-            look_up(step, (0, 1))
-            smaller_on_vector(2 * step, [step], 0, BANK)
-            smaller_on_vector(2 * step + 1, [step], BANK, T - SLIVER - BANK)
+        nc.vector.tensor_copy(old[:, 1, :], store[1][:].indirect(offsets[:]))
+        smaller_on_vector(0, [0], 0, BANK)
+        y = psum.tile([P, BANK], F32, name="bank1")
+        rest = ((0, BANK, y[:, : T - SLIVER - BANK]), (1, MASKED[1], y[:, T - SLIVER - BANK :]))
+        for step, first, part in rest:
+            project(part, step, first, T - SLIVER - first)
+        for step, first, part in rest:
+            cols = slice(first, T - SLIVER)
+            nc.vector.tensor_tensor(new[:, step, cols], old[:, step, cols], part, ALU.min)
 
-        minus_y = {step: keep.tile([P, MASKED], F32, name="minus_y%d" % step) for step in MASKED_STEPS}
-        keep_old = {step: keep.tile([P, MASKED], F32, name="keep_old%d" % step) for step in MASKED_STEPS}
-        take_new = {step: keep.tile([P, MASKED], F32, name="take_new%d" % step) for step in MASKED_STEPS}
-        signs = shared.tile([P, U * PACK], BF16, name="signs", align_bytes=64, offset=0)
-        minus_half = signs[:, BANK : BANK + 1]
+        minus_y = {step: old[:, step + 3, : MASKED[step]] for step in MASKED_STEPS}
+        choice = {step: keep.tile([P, 2, MASKED[step]], F32, name="masks%d" % step) for step in MASKED_STEPS}
+        keep_old = {step: choice[step][:, 0, :] for step in MASKED_STEPS}
+        take_new = {step: choice[step][:, 1, :] for step in MASKED_STEPS}
+        signs = shared.tile([P, U * 2], BF16, name="signs", align_bytes=64, offset=0)
+        minus_half = signs[:, 2 * U - 1 : 2 * U]
         nc.vector.memset(minus_half, -0.5)
         first_piece_bank = 2 * len(VECTOR_STEPS)
 
@@ -136,7 +145,7 @@ def tile_picked_widxput_min_lo_kernel(tc, x_words, x_scales, mem, w1, slot, out_
                 block = slice(first + P * b, first + P * (b + 1))
                 nc.tensor.matmul(gap[:, P * b : P * (b + 1)], old[:, step, block], ident_f32[:], start=True, stop=False, is_transpose=True)
                 nc.tensor.matmul(gap[:, P * b : P * (b + 1)], minus_y[step][:, block], ident_f32[:], start=False, stop=True, is_transpose=True)
-            turned = signs[:, U * i : U * i + width]
+            turned = signs[:, BANK * i : BANK * i + width]
             nc.scalar.activation(turned, gap[:], ACT.Sign)
             side = psum.tile([P, width], BF16, name="bank%d" % (first_piece_bank + i))
             for b in range(width // P):
@@ -147,43 +156,55 @@ def tile_picked_widxput_min_lo_kernel(tc, x_words, x_scales, mem, w1, slot, out_
         for i in range(len(PIECES)):
             fetch_y(i)
         nc.vector.tensor_copy(old[:, 2, :], store[2][:].indirect(offsets[:]))
-        look_up(3, (1, 0))
+        look_up(3, BANK, BANK)
+        look_up(3, BANK // 2, BANK // 2)
         smaller_on_vector(0, range(PACK), T - SLIVER, SLIVER)
-        smaller_on_vector(1, MASKED_STEPS, MASKED, SLIVER)
+        look_up(3, 0, BANK // 2)
         for i in range(len(PIECES)):
             make_masks(i)
         for step in MASKED_STEPS:
-            nc.gpsimd.tensor_tensor(keep_old[step][:], keep_old[step][:], old[:, step, :MASKED], ALU.mult)
-            nc.gpsimd.tensor_tensor(take_new[step][:], take_new[step][:], minus_y[step][:], ALU.mult)
-            nc.gpsimd.tensor_tensor(new[:, step, :MASKED], keep_old[step][:], take_new[step][:], ALU.add)
+            products = old[:, 0 : 2 * PACK : 2 * PACK - 1, T - MASKED[step] :]
+            parts = (slice(MASKED[step] // 2, MASKED[step]), slice(0, MASKED[step] // 2))
+            for part in parts:
+                nc.gpsimd.tensor_tensor(products[:, :, part], choice[step][:, :, part], old[:, step : step + 4 : 3, part], ALU.mult)
+            for part in parts:
+                nc.gpsimd.tensor_tensor(new[:, step, part], products[:, 0, part], products[:, 1, part], ALU.add)
 
-        rounded = [shared.tile([P, width, PACK], BF16, name="rounded%d" % c, align_bytes=64, offset=2 * PACK * first) for c, (first, width, on_vector) in enumerate(CHUNKS)]
+        pairs = shared.tile([P, U, 2], BF16, name="pairs", align_bytes=64, offset=0)
+        pair_words = pairs[:].rearrange("p c t -> p (c t)").bitcast(U32)
+        rounded = [keep.tile([P, width, PACK], BF16, name="rounded%d" % c, align_bytes=64) for c, (first, width, on_vector) in enumerate(CHUNKS)]
         words = keep.tile([P, U], U32, name="words", align_bytes=64)
         plane = keep.tile([P, GROUP], U8, name="plane", align_bytes=64)
 
         for step, t in enumerate(ORDER):
             nc.vector.tensor_copy(store[step][:].indirect(offsets[:]), new[:, step, :])
             nc.sync.dma_start(out_rows[:, t, :], store[step][:])
-            last = step == PACK - 1
-            for c, (first, width, on_vector) in enumerate(CHUNKS):
-                if last and on_vector:
-                    nc.vector.tensor_copy(rounded[c][:, :, t], store[step][:, first : first + width])
+            if step < 2:
+                nc.scalar.copy(pairs[:, :, t], store[step][:])
             for c, (first, width, on_vector) in enumerate(CHUNKS):
                 values = store[step][:, first : first + width]
-                on_pool = first >= POOL_FROM
-                if (step == 0 and on_vector) or (step == 1 and on_pool):
-                    nc.scalar.copy(rounded[c][:, :, t : t + 2], values.unsqueeze(2).to_broadcast([P, width, 2]))
+                both = values.unsqueeze(2).to_broadcast([P, width, 2])
+                on_pool = POOL_FROM <= first
+                if step == 1:
+                    as_words = rounded[c][:].rearrange("p c t -> p (c t)").bitcast(U32).rearrange("p (c u) -> p c u", u=2)
+                    nc.scalar.copy(as_words, pair_words[:, first : first + width].unsqueeze(2).to_broadcast([P, width, 2]))
                 elif step == 2 and on_pool:
-                    nc.gpsimd.tensor_scalar(rounded[c][:, :, t], values, 1.0, -0.0, ALU.mult, ALU.add)
-                elif not (last and on_vector):
+                    nc.gpsimd.tensor_scalar(rounded[c][:, :, 2:], both, 1.0, -0.0, ALU.mult, ALU.add)
+                elif step == 2 and on_vector:
+                    nc.scalar.copy(rounded[c][:, :, 2:], both)
+                elif step == 3 and on_vector:
+                    nc.vector.tensor_copy(rounded[c][:, :, t], values)
+                elif step >= 2:
                     nc.scalar.copy(rounded[c][:, :, t], values)
 
-        for c, (first, width, on_vector) in enumerate(CHUNKS):
+        for first, width in CALLS:
+            c = [i for i, chunk in enumerate(CHUNKS) if chunk[0] <= first < chunk[0] + chunk[1]][0]
+            inside = first - CHUNKS[c][0]
             group, col = divmod(first, GROUP)
             nc.vector.quantize_mx(
                 out=words[:, first : first + width].bitcast(FP8X4),
                 scales=plane[4 * group :, col : col + width],
-                in_=rounded[c][:].rearrange("p c t -> p (c t)"),
+                in_=rounded[c][:, inside : inside + width].rearrange("p c t -> p (c t)"),
             )
         for first, width in WORD_STORES:
             nc.sync.dma_start(out_words[:, first : first + width], words[:, first : first + width].bitcast(I32))

@@ -51,13 +51,15 @@ def tile_picked_widxput_min_lo_kernel(tc, x_words, x_scales, mem, w1, slot, out_
 
         offsets = keep.tile([P, T // LANES], U16, name="offsets")
         store = [keep.tile([P, U], F32, name="store%d" % step) for step in range(PACK)]
-        w_raw = keep.tile([P, PACK, N], F32, name="w_raw")
+        old = keep.tile([P, 2 * PACK, T], F32, name="old")
+        new = keep.tile([P, PACK, T], F32, name="new")
+        w_raw = old[:, 1:3, :].rearrange("p r (h c) -> p (r h) c", c=N)
         x_plane = keep.tile([P, T], U8, name="x_plane", align_bytes=64)
         x_codes = keep.tile([P, 2 * T], U8, name="x_codes", align_bytes=64)
         nc.vector.memset(x_plane[:].bitcast(I32), 0)
         nc.sync.dma_start(offsets[:], slot)
         nc.sync.dma_start(store[0][:], mem_rows[:, ORDER[0], :])
-        nc.sync.dma_start(w_raw[:], w1.rearrange("(p j) c -> p j c", j=PACK))
+        nc.sync.dma_start(w_raw, w1.rearrange("(p j) c -> p j c", j=PACK))
         nc.sync.dma_start(store[1][:], mem_rows[:, ORDER[1], :])
         nc.sync.dma_start(x_codes[:].bitcast(I32), x_words[0].bitcast(I32))
         for q in range(QUADRANTS):
@@ -70,13 +72,10 @@ def tile_picked_widxput_min_lo_kernel(tc, x_words, x_scales, mem, w1, slot, out_
         make_identity(nc, ident_f32[:])
         make_identity(nc, ident_bf16[:])
 
-        old = keep.tile([P, 2 * PACK, T], F32, name="old", align_bytes=64)
-        new = keep.tile([P, PACK, T], F32, name="new")
-
         nc.vector.tensor_copy(old[:, 0, :], store[0][:].indirect(offsets[:]))
 
-        w_by_m = w_raw[:].rearrange("p j (m t) -> p m t j", t=PACK)
-        w_round = [old[:, 1, BANK * h : BANK * (h + 1)].bitcast(BF16).rearrange("p (t m j) -> p t m j", t=2, j=PACK) for h in range(2)]
+        w_by_m = w_raw.rearrange("p j (m t) -> p m t j", t=PACK)
+        w_round = [keep.tile([P, 2, P, PACK], BF16, name="w_round%d" % h, align_bytes=64)[:] for h in range(2)]
         w_round_by_m = [half.rearrange("p t m j -> p m t j") for half in w_round]
         w_codes = [keep.tile([P, P], U32, name="w_codes%d" % step, align_bytes=64) for step in range(PACK)]
         w_plane = [keep.tile([P, P], U8, name="w_plane%d" % step, align_bytes=64) for step in range(PACK)]
@@ -153,14 +152,18 @@ def tile_picked_widxput_min_lo_kernel(tc, x_words, x_scales, mem, w1, slot, out_
             nc.scalar.activation(keep_old[step][:, cols], side[:], ACT.Copy, scale=-0.5, bias=0.5)
             nc.scalar.activation(take_new[step][:, cols], side[:], ACT.Identity, scale=-0.5, bias=minus_half)
 
-        for i in range(len(PIECES)):
+        for i in range(2):
+            fetch_y(i)
+        for i in range(2):
+            make_masks(i)
+        for i in range(2, len(PIECES)):
             fetch_y(i)
         nc.vector.tensor_copy(old[:, 2, :], store[2][:].indirect(offsets[:]))
         look_up(3, BANK, BANK)
         look_up(3, BANK // 2, BANK // 2)
         smaller_on_vector(0, range(PACK), T - SLIVER, SLIVER)
         look_up(3, 0, BANK // 2)
-        for i in range(len(PIECES)):
+        for i in range(2, len(PIECES)):
             make_masks(i)
         for step in MASKED_STEPS:
             products = old[:, 0 : 2 * PACK : 2 * PACK - 1, T - MASKED[step] :]
@@ -181,7 +184,7 @@ def tile_picked_widxput_min_lo_kernel(tc, x_words, x_scales, mem, w1, slot, out_
             nc.sync.dma_start(out_rows[:, t, :], store[step][:])
             if step < 2:
                 nc.scalar.copy(pairs[:, :, t], store[step][:])
-            for c, (first, width, on_vector) in enumerate(CHUNKS):
+            for c, (first, width, on_vector) in sorted(enumerate(CHUNKS), reverse=step == 1):
                 values = store[step][:, first : first + width]
                 both = values.unsqueeze(2).to_broadcast([P, width, 2])
                 on_pool = POOL_FROM <= first

@@ -25,12 +25,11 @@ QUADRANTS = 4
 GROUP = 512
 
 ORDER = (0, 1, 2, 3)
-VECTOR_STEPS = (0,)
 MASKED_STEPS = (1, 2, 3)
 SLIVER = 128
-MASKED = {1: T - 2 * SLIVER, 2: T - SLIVER, 3: T - SLIVER}
-PIECES = tuple((step, first, width) for step in MASKED_STEPS for first, width in ((0, MASKED[step] - BANK), (MASKED[step] - BANK, BANK)))
-W_ON_SCALAR = 80
+BEHIND = BANK + SLIVER
+PIECES = tuple(piece for step in MASKED_STEPS for piece in ((step, BEHIND, T - BEHIND), (step, SLIVER * (step == 1), BANK - SLIVER * (step == 1))))
+W_ON_SCALAR = 40
 POOL_FROM = 1536
 
 CHUNKS = [(0, 512, True), (512, 384, True), (896, 384, False), (1280, 256, False), (1536, 256, False), (1792, 256, False)]
@@ -51,16 +50,19 @@ def tile_picked_widxput_min_lo_kernel(tc, x_words, x_scales, mem, w1, slot, out_
 
         offsets = keep.tile([P, T // LANES], U16, name="offsets")
         store = [keep.tile([P, U], F32, name="store%d" % step) for step in range(PACK)]
-        old = keep.tile([P, 2 * PACK, T], F32, name="old")
+        rows = keep.tile([P, 2 * PACK, T], F32, name="rows")
+        old = rows[:, 1:, :]
         new = keep.tile([P, PACK, T], F32, name="new")
-        w_raw = old[:, 1:3, :].rearrange("p r (h c) -> p (r h) c", c=N)
+        old_flat = old.rearrange("p r c -> p (r c)")
+        new_flat = new[:].rearrange("p r c -> p (r c)")
+        w_raw = rows[:, :2, :].rearrange("p r (h c) -> p (r h) c", c=N)
         x_plane = keep.tile([P, T], U8, name="x_plane", align_bytes=64)
         x_codes = keep.tile([P, 2 * T], U8, name="x_codes", align_bytes=64)
         nc.vector.memset(x_plane[:].bitcast(I32), 0)
-        nc.sync.dma_start(offsets[:], slot)
-        nc.sync.dma_start(store[0][:], mem_rows[:, ORDER[0], :])
-        nc.sync.dma_start(w_raw, w1.rearrange("(p j) c -> p j c", j=PACK))
         nc.sync.dma_start(store[1][:], mem_rows[:, ORDER[1], :])
+        nc.sync.dma_start(offsets[:], slot)
+        nc.sync.dma_start(w_raw, w1.rearrange("(p j) c -> p j c", j=PACK))
+        nc.sync.dma_start(store[0][:], mem_rows[:, ORDER[0], :])
         nc.sync.dma_start(x_codes[:].bitcast(I32), x_words[0].bitcast(I32))
         for q in range(QUADRANTS):
             nc.sync.dma_start(x_plane[32 * q : 32 * q + 4, :].bitcast(I32), x_scales[0, 4 * q : 4 * q + 4, :].bitcast(I32))
@@ -72,18 +74,18 @@ def tile_picked_widxput_min_lo_kernel(tc, x_words, x_scales, mem, w1, slot, out_
         make_identity(nc, ident_f32[:])
         make_identity(nc, ident_bf16[:])
 
-        nc.vector.tensor_copy(old[:, 0, :], store[0][:].indirect(offsets[:]))
+        nc.vector.tensor_copy(old[:, 1, :], store[1][:].indirect(offsets[:]))
 
         w_by_m = w_raw.rearrange("p j (m t) -> p m t j", t=PACK)
-        w_round = [keep.tile([P, 2, P, PACK], BF16, name="w_round%d" % h, align_bytes=64)[:] for h in range(2)]
-        w_round_by_m = [half.rearrange("p t m j -> p m t j") for half in w_round]
-        w_codes = [keep.tile([P, P], U32, name="w_codes%d" % step, align_bytes=64) for step in range(PACK)]
-        w_plane = [keep.tile([P, P], U8, name="w_plane%d" % step, align_bytes=64) for step in range(PACK)]
-        nc.vector.tensor_copy(w_round_by_m[0], w_by_m[:, :, :2])
-        nc.scalar.copy(w_round_by_m[1][:, :W_ON_SCALAR], w_by_m[:, :W_ON_SCALAR, 2:])
-        nc.vector.tensor_copy(w_round_by_m[1][:, W_ON_SCALAR:], w_by_m[:, W_ON_SCALAR:, 2:])
-        for step, t in enumerate(ORDER):
-            nc.vector.quantize_mx(out=w_codes[step][:].bitcast(FP8X4), scales=w_plane[step][:], in_=w_round[t // 2][:, t % 2].rearrange("p m j -> p (m j)"))
+        w_round = keep.tile([P, PACK, P, PACK], BF16, name="w_round", align_bytes=64)
+        w_round_by_m = w_round[:].rearrange("p t m j -> p m t j")
+        all_codes = keep.tile([P, N], U32, name="w_codes", align_bytes=64)
+        all_planes = keep.tile([P, N], U8, name="w_plane", align_bytes=64)
+        w_codes = [all_codes[:, P * t : P * (t + 1)] for t in ORDER]
+        w_plane = [all_planes[:, P * t : P * (t + 1)] for t in ORDER]
+        nc.scalar.copy(w_round_by_m[:, :W_ON_SCALAR], w_by_m[:, :W_ON_SCALAR])
+        nc.vector.tensor_copy(w_round_by_m[:, W_ON_SCALAR:], w_by_m[:, W_ON_SCALAR:])
+        nc.vector.quantize_mx(out=all_codes[:].bitcast(FP8X4), scales=all_planes[:], in_=w_round[:].rearrange("p t m j -> p (t m j)"))
 
         def project(out, step, first, width):
             done = 0
@@ -92,8 +94,8 @@ def tile_picked_widxput_min_lo_kernel(tc, x_words, x_scales, mem, w1, slot, out_
                     start = first + done
                     nc.tensor.matmul_mx(
                         out=out[:, done : done + count],
-                        lhsT=w_codes[step][:].bitcast(FP8X4),
-                        lhsT_scale=w_plane[step][:],
+                        lhsT=w_codes[step].bitcast(FP8X4),
+                        lhsT_scale=w_plane[step],
                         rhs=x_codes[:, 2 * start : 2 * (start + count)].bitcast(FP4X4),
                         rhs_scale=x_plane[:, start : start + count],
                         start=True,
@@ -105,48 +107,46 @@ def tile_picked_widxput_min_lo_kernel(tc, x_words, x_scales, mem, w1, slot, out_
             y = psum.tile([P, len(steps), width], F32, name="bank%d" % bank)
             for i, step in enumerate(steps):
                 project(y[:, i, :], step, first, width)
-            rows, cols = slice(steps[0], steps[-1] + 1), slice(first, first + width)
-            nc.vector.tensor_tensor(new[:, rows, cols], old[:, rows, cols], y[:], ALU.min)
+            among, cols = slice(steps[0], steps[-1] + 1), slice(first, first + width)
+            nc.vector.tensor_tensor(new[:, among, cols], old[:, among, cols], y[:], ALU.min)
 
         def look_up(step, first, width):
             nc.vector.tensor_copy(old[:, step, first : first + width], store[step][:].indirect(offsets[:, first // LANES : (first + width) // LANES]))
 
-        nc.vector.tensor_copy(old[:, 1, :], store[1][:].indirect(offsets[:]))
+        look_up(0, 0, BANK)
+        look_up(0, BANK, BANK)
         smaller_on_vector(0, [0], 0, BANK)
         y = psum.tile([P, BANK], F32, name="bank1")
-        rest = ((0, BANK, y[:, : T - SLIVER - BANK]), (1, MASKED[1], y[:, T - SLIVER - BANK :]))
-        for step, first, part in rest:
-            project(part, step, first, T - SLIVER - first)
-        for step, first, part in rest:
-            cols = slice(first, T - SLIVER)
-            nc.vector.tensor_tensor(new[:, step, cols], old[:, step, cols], part, ALU.min)
+        project(y[:, : T - BEHIND], 0, BEHIND, T - BEHIND)
+        project(y[:, T - BEHIND :], 1, 0, SLIVER)
+        nc.vector.tensor_tensor(new_flat[:, BEHIND : T + SLIVER], old_flat[:, BEHIND : T + SLIVER], y[:], ALU.min)
 
-        minus_y = {step: old[:, step + 3, : MASKED[step]] for step in MASKED_STEPS}
-        choice = {step: keep.tile([P, 2, MASKED[step]], F32, name="masks%d" % step) for step in MASKED_STEPS}
+        minus_y = {step: old[:, step + 3, :] for step in MASKED_STEPS}
+        choice = {step: keep.tile([P, 2, T], F32, name="masks%d" % step) for step in MASKED_STEPS}
         keep_old = {step: choice[step][:, 0, :] for step in MASKED_STEPS}
         take_new = {step: choice[step][:, 1, :] for step in MASKED_STEPS}
         signs = shared.tile([P, U * 2], BF16, name="signs", align_bytes=64, offset=0)
         minus_half = signs[:, 2 * U - 1 : 2 * U]
         nc.vector.memset(minus_half, -0.5)
-        first_piece_bank = 2 * len(VECTOR_STEPS)
+        piece_bank = (2, 3, 0, 1, 2, 3)
 
         def fetch_y(i):
             step, first, width = PIECES[i]
-            y = psum.tile([P, width], F32, name="bank%d" % (first_piece_bank + i))
+            y = psum.tile([P, width], F32, name="bank%d" % piece_bank[i])
             project(y[:], step, first, width)
             nc.scalar.activation(minus_y[step][:, first : first + width], y[:], ACT.Copy, scale=-1.0)
 
         def make_masks(i):
             step, first, width = PIECES[i]
             cols = slice(first, first + width)
-            gap = psum.tile([P, width], F32, name="bank%d" % (first_piece_bank + i))
+            gap = psum.tile([P, width], F32, name="bank%d" % piece_bank[i])
             for b in range(width // P):
                 block = slice(first + P * b, first + P * (b + 1))
                 nc.tensor.matmul(gap[:, P * b : P * (b + 1)], old[:, step, block], ident_f32[:], start=True, stop=False, is_transpose=True)
                 nc.tensor.matmul(gap[:, P * b : P * (b + 1)], minus_y[step][:, block], ident_f32[:], start=False, stop=True, is_transpose=True)
             turned = signs[:, BANK * i : BANK * i + width]
             nc.scalar.activation(turned, gap[:], ACT.Sign)
-            side = psum.tile([P, width], BF16, name="bank%d" % (first_piece_bank + i))
+            side = psum.tile([P, width], BF16, name="bank%d" % piece_bank[i])
             for b in range(width // P):
                 nc.tensor.transpose(side[:, P * b : P * (b + 1)], turned[:, P * b : P * (b + 1)], ident_bf16[:])
             nc.scalar.activation(keep_old[step][:, cols], side[:], ACT.Copy, scale=-0.5, bias=0.5)
@@ -156,22 +156,24 @@ def tile_picked_widxput_min_lo_kernel(tc, x_words, x_scales, mem, w1, slot, out_
             fetch_y(i)
         for i in range(2):
             make_masks(i)
-        for i in range(2, len(PIECES)):
+        for i in range(2, 4):
             fetch_y(i)
         nc.vector.tensor_copy(old[:, 2, :], store[2][:].indirect(offsets[:]))
-        look_up(3, BANK, BANK)
-        look_up(3, BANK // 2, BANK // 2)
-        smaller_on_vector(0, range(PACK), T - SLIVER, SLIVER)
-        look_up(3, 0, BANK // 2)
+        look_up(3, BANK, BANK // 2)
+        look_up(3, 0, BANK)
+        smaller_on_vector(4, range(PACK), BANK, SLIVER)
+        look_up(3, T - BANK // 2, BANK // 2)
+        for i in range(4, 6):
+            fetch_y(i)
         for i in range(2, len(PIECES)):
             make_masks(i)
+        middle = BANK + SLIVER // 2
         for step in MASKED_STEPS:
-            products = old[:, 0 : 2 * PACK : 2 * PACK - 1, T - MASKED[step] :]
-            parts = (slice(MASKED[step] // 2, MASKED[step]), slice(0, MASKED[step] // 2))
-            for part in parts:
-                nc.gpsimd.tensor_tensor(products[:, :, part], choice[step][:, :, part], old[:, step : step + 4 : 3, part], ALU.mult)
-            for part in parts:
-                nc.gpsimd.tensor_tensor(new[:, step, part], products[:, 0, part], products[:, 1, part], ALU.add)
+            parts = [(slice(first, first + width), rows[:, :2, room : room + width]) for (of, first, width), room in zip(PIECES[2 * step - 2 : 2 * step], (middle, middle - PIECES[2 * step - 1][2]))]
+            for part, products in parts:
+                nc.gpsimd.tensor_tensor(products, choice[step][:, :, part], old[:, step : step + 4 : 3, part], ALU.mult)
+            for part, products in parts:
+                nc.gpsimd.tensor_tensor(new[:, step, part], products[:, 0, :], products[:, 1, :], ALU.add)
 
         pairs = shared.tile([P, U, 2], BF16, name="pairs", align_bytes=64, offset=0)
         pair_words = pairs[:].rearrange("p c t -> p (c t)").bitcast(U32)

@@ -26,9 +26,9 @@ GROUP = 512
 
 ORDER = (0, 1, 2, 3)
 MASKED_STEPS = (1, 2, 3)
+ROW = {1: 0, 0: 1, 2: 2, 3: 3}
 SLIVER = 128
-BEHIND = BANK + SLIVER
-PIECES = tuple(piece for step in MASKED_STEPS for piece in ((step, BEHIND, T - BEHIND), (step, SLIVER * (step == 1), BANK - SLIVER * (step == 1))))
+PIECES = ((1, 0, 384, 2), (1, 384, 512, 3), (2, 0, 384, 0), (2, 384, 512, 1), (3, 0, 512, 2), (3, 512, 384, 3))
 W_ON_SCALAR = 40
 POOL_FROM = 1536
 
@@ -50,12 +50,9 @@ def tile_picked_widxput_min_lo_kernel(tc, x_words, x_scales, mem, w1, slot, out_
 
         offsets = keep.tile([P, T // LANES], U16, name="offsets")
         store = [keep.tile([P, U], F32, name="store%d" % step) for step in range(PACK)]
-        rows = keep.tile([P, 2 * PACK, T], F32, name="rows")
-        old = rows[:, 1:, :]
+        old = keep.tile([P, 2 * PACK, T], F32, name="old")
         new = keep.tile([P, PACK, T], F32, name="new")
-        old_flat = old.rearrange("p r c -> p (r c)")
-        new_flat = new[:].rearrange("p r c -> p (r c)")
-        w_raw = rows[:, :2, :].rearrange("p r (h c) -> p (r h) c", c=N)
+        w_raw = old[:, ROW[0] : ROW[0] + 2, :].rearrange("p r (h c) -> p (r h) c", c=N)
         x_plane = keep.tile([P, T], U8, name="x_plane", align_bytes=64)
         x_codes = keep.tile([P, 2 * T], U8, name="x_codes", align_bytes=64)
         nc.vector.memset(x_plane[:].bitcast(I32), 0)
@@ -74,7 +71,7 @@ def tile_picked_widxput_min_lo_kernel(tc, x_words, x_scales, mem, w1, slot, out_
         make_identity(nc, ident_f32[:])
         make_identity(nc, ident_bf16[:])
 
-        nc.vector.tensor_copy(old[:, 1, :], store[1][:].indirect(offsets[:]))
+        nc.vector.tensor_copy(old[:, ROW[1], :], store[1][:].indirect(offsets[:]))
 
         w_by_m = w_raw.rearrange("p j (m t) -> p m t j", t=PACK)
         w_round = keep.tile([P, PACK, P, PACK], BF16, name="w_round", align_bytes=64)
@@ -107,73 +104,68 @@ def tile_picked_widxput_min_lo_kernel(tc, x_words, x_scales, mem, w1, slot, out_
             y = psum.tile([P, len(steps), width], F32, name="bank%d" % bank)
             for i, step in enumerate(steps):
                 project(y[:, i, :], step, first, width)
-            among, cols = slice(steps[0], steps[-1] + 1), slice(first, first + width)
-            nc.vector.tensor_tensor(new[:, among, cols], old[:, among, cols], y[:], ALU.min)
+            rows, cols = slice(ROW[steps[0]], ROW[steps[-1]] + 1), slice(first, first + width)
+            nc.vector.tensor_tensor(new[:, rows, cols], old[:, rows, cols], y[:], ALU.min)
 
         def look_up(step, first, width):
-            nc.vector.tensor_copy(old[:, step, first : first + width], store[step][:].indirect(offsets[:, first // LANES : (first + width) // LANES]))
+            nc.vector.tensor_copy(old[:, ROW[step], first : first + width], store[step][:].indirect(offsets[:, first // LANES : (first + width) // LANES]))
 
-        look_up(0, 0, BANK)
-        look_up(0, BANK, BANK)
-        smaller_on_vector(0, [0], 0, BANK)
-        y = psum.tile([P, BANK], F32, name="bank1")
-        project(y[:, : T - BEHIND], 0, BEHIND, T - BEHIND)
-        project(y[:, T - BEHIND :], 1, 0, SLIVER)
-        nc.vector.tensor_tensor(new_flat[:, BEHIND : T + SLIVER], old_flat[:, BEHIND : T + SLIVER], y[:], ALU.min)
 
-        minus_y = {step: old[:, step + 3, :] for step in MASKED_STEPS}
-        choice = {step: keep.tile([P, 2, T], F32, name="masks%d" % step) for step in MASKED_STEPS}
+        minus_y = {step: old[:, ROW[step] + PACK, :] for step in MASKED_STEPS}
+        choice = {step: keep.tile([P, 2, T], F32, name="choice%d" % step) for step in MASKED_STEPS}
         keep_old = {step: choice[step][:, 0, :] for step in MASKED_STEPS}
         take_new = {step: choice[step][:, 1, :] for step in MASKED_STEPS}
         signs = shared.tile([P, U * 2], BF16, name="signs", align_bytes=64, offset=0)
         minus_half = signs[:, 2 * U - 1 : 2 * U]
         nc.vector.memset(minus_half, -0.5)
-        piece_bank = (2, 3, 0, 1, 2, 3)
 
         def fetch_y(i):
-            step, first, width = PIECES[i]
-            y = psum.tile([P, width], F32, name="bank%d" % piece_bank[i])
+            step, first, width, bank = PIECES[i]
+            y = psum.tile([P, width], F32, name="bank%d" % bank)
             project(y[:], step, first, width)
             nc.scalar.activation(minus_y[step][:, first : first + width], y[:], ACT.Copy, scale=-1.0)
 
         def make_masks(i):
-            step, first, width = PIECES[i]
+            step, first, width, bank = PIECES[i]
             cols = slice(first, first + width)
-            gap = psum.tile([P, width], F32, name="bank%d" % piece_bank[i])
+            gap = psum.tile([P, width], F32, name="bank%d" % bank)
             for b in range(width // P):
                 block = slice(first + P * b, first + P * (b + 1))
-                nc.tensor.matmul(gap[:, P * b : P * (b + 1)], old[:, step, block], ident_f32[:], start=True, stop=False, is_transpose=True)
+                nc.tensor.matmul(gap[:, P * b : P * (b + 1)], old[:, ROW[step], block], ident_f32[:], start=True, stop=False, is_transpose=True)
                 nc.tensor.matmul(gap[:, P * b : P * (b + 1)], minus_y[step][:, block], ident_f32[:], start=False, stop=True, is_transpose=True)
             turned = signs[:, BANK * i : BANK * i + width]
             nc.scalar.activation(turned, gap[:], ACT.Sign)
-            side = psum.tile([P, width], BF16, name="bank%d" % piece_bank[i])
+            side = psum.tile([P, width], BF16, name="bank%d" % bank)
             for b in range(width // P):
                 nc.tensor.transpose(side[:, P * b : P * (b + 1)], turned[:, P * b : P * (b + 1)], ident_bf16[:])
             nc.scalar.activation(keep_old[step][:, cols], side[:], ACT.Copy, scale=-0.5, bias=0.5)
             nc.scalar.activation(take_new[step][:, cols], side[:], ACT.Identity, scale=-0.5, bias=minus_half)
 
-        for i in range(2):
+        of_step = {step: [i for i, piece in enumerate(PIECES) if piece[0] == step] for step in MASKED_STEPS}
+        look_up(0, 0, BANK)
+        look_up(0, BANK, BANK)
+        smaller_on_vector(0, [0], 0, BANK)
+        smaller_on_vector(1, [0], BANK, T - SLIVER - BANK)
+        for i in of_step[1]:
             fetch_y(i)
-        for i in range(2):
+        for i in of_step[1]:
             make_masks(i)
-        for i in range(2, 4):
+        for i in of_step[2]:
             fetch_y(i)
-        nc.vector.tensor_copy(old[:, 2, :], store[2][:].indirect(offsets[:]))
-        look_up(3, BANK, BANK // 2)
-        look_up(3, 0, BANK)
-        smaller_on_vector(4, range(PACK), BANK, SLIVER)
+        look_up(2, 0, T)
         look_up(3, T - BANK // 2, BANK // 2)
-        for i in range(4, 6):
+        look_up(3, 0, BANK)
+        smaller_on_vector(4, [1, 0, 2, 3], T - SLIVER, SLIVER)
+        look_up(3, BANK, BANK // 2)
+        for i in of_step[3]:
             fetch_y(i)
-        for i in range(2, len(PIECES)):
+        for i in of_step[2] + of_step[3]:
             make_masks(i)
-        middle = BANK + SLIVER // 2
-        for step in MASKED_STEPS:
-            parts = [(slice(first, first + width), rows[:, :2, room : room + width]) for (of, first, width), room in zip(PIECES[2 * step - 2 : 2 * step], (middle, middle - PIECES[2 * step - 1][2]))]
-            for part, products in parts:
-                nc.gpsimd.tensor_tensor(products, choice[step][:, :, part], old[:, step : step + 4 : 3, part], ALU.mult)
-            for part, products in parts:
-                nc.gpsimd.tensor_tensor(new[:, step, part], products[:, 0, :], products[:, 1, :], ALU.add)
+        products = keep.tile([P, 2, T], F32, name="products")
+        parts = [(1, slice(PIECES[i][1], PIECES[i][1] + PIECES[i][2])) for i in of_step[1]] + [(step, slice(0, T - SLIVER)) for step in MASKED_STEPS[1:]]
+        for step, part in parts:
+            nc.gpsimd.tensor_tensor(products[:, :, part], choice[step][:, :, part], old[:, ROW[step] : ROW[step] + PACK + 1 : PACK, part], ALU.mult)
+            nc.gpsimd.tensor_tensor(new[:, ROW[step], part], products[:, 0, part], products[:, 1, part], ALU.add)
 
         pairs = shared.tile([P, U, 2], BF16, name="pairs", align_bytes=64, offset=0)
         pair_words = pairs[:].rearrange("p c t -> p (c t)").bitcast(U32)
@@ -182,7 +174,7 @@ def tile_picked_widxput_min_lo_kernel(tc, x_words, x_scales, mem, w1, slot, out_
         plane = keep.tile([P, GROUP], U8, name="plane", align_bytes=64)
 
         for step, t in enumerate(ORDER):
-            nc.vector.tensor_copy(store[step][:].indirect(offsets[:]), new[:, step, :])
+            nc.vector.tensor_copy(store[step][:].indirect(offsets[:]), new[:, ROW[step], :])
             nc.sync.dma_start(out_rows[:, t, :], store[step][:])
             if step < 2:
                 nc.scalar.copy(pairs[:, :, t], store[step][:])

@@ -26,9 +26,10 @@ GROUP = 512
 
 ORDER = (0, 1, 2, 3)
 MASKED_STEPS = (1, 2, 3)
-ROW = {1: 0, 0: 1, 2: 2, 3: 3}
+ROW = {1: 0, 0: 1, 3: 2, 2: 3}
 SLIVER = 128
-PIECES = ((1, 0, 384, 2), (1, 384, 512, 3), (2, 0, 384, 0), (2, 384, 512, 1), (3, 0, 512, 2), (3, 512, 384, 3))
+PIECES = ((1, 0, 256, 2), (1, 256, 384, 3), (1, 640, 384, 5), (2, 0, 512, 0), (2, 512, 512, 1), (3, 0, 512, 3), (3, 512, 384, 5))
+ROUNDS = ((1, (0, 256)), (1, (256, 640, T)), (2, (0, BANK, T)), (3, (0, T - SLIVER)))
 W_ON_SCALAR = 40
 POOL_FROM = 1536
 
@@ -100,11 +101,13 @@ def tile_picked_widxput_min_lo_kernel(tc, x_words, x_scales, mem, w1, slot, out_
                     )
                     done = done + count
 
-        def smaller_on_vector(bank, steps, first, width):
+        def project_for_vector(bank, steps, first, width):
             y = psum.tile([P, len(steps), width], F32, name="bank%d" % bank)
             for i, step in enumerate(steps):
                 project(y[:, i, :], step, first, width)
-            rows, cols = slice(ROW[steps[0]], ROW[steps[-1]] + 1), slice(first, first + width)
+            return y, slice(ROW[steps[0]], ROW[steps[-1]] + 1), slice(first, first + width)
+
+        def smaller_on_vector(y, rows, cols):
             nc.vector.tensor_tensor(new[:, rows, cols], old[:, rows, cols], y[:], ALU.min)
 
         def look_up(step, first, width):
@@ -125,6 +128,10 @@ def tile_picked_widxput_min_lo_kernel(tc, x_words, x_scales, mem, w1, slot, out_
             project(y[:], step, first, width)
             nc.scalar.activation(minus_y[step][:, first : first + width], y[:], ACT.Copy, scale=-1.0)
 
+        def masks_from(sign, step, cols):
+            nc.scalar.activation(keep_old[step][:, cols], sign, ACT.Copy, scale=-0.5, bias=0.5)
+            nc.scalar.activation(take_new[step][:, cols], sign, ACT.Identity, scale=-0.5, bias=minus_half)
+
         def make_masks(i):
             step, first, width, bank = PIECES[i]
             cols = slice(first, first + width)
@@ -138,34 +145,42 @@ def tile_picked_widxput_min_lo_kernel(tc, x_words, x_scales, mem, w1, slot, out_
             side = psum.tile([P, width], BF16, name="bank%d" % bank)
             for b in range(width // P):
                 nc.tensor.transpose(side[:, P * b : P * (b + 1)], turned[:, P * b : P * (b + 1)], ident_bf16[:])
-            nc.scalar.activation(keep_old[step][:, cols], side[:], ACT.Copy, scale=-0.5, bias=0.5)
-            nc.scalar.activation(take_new[step][:, cols], side[:], ACT.Identity, scale=-0.5, bias=minus_half)
+            masks_from(side[:], step, cols)
 
         of_step = {step: [i for i, piece in enumerate(PIECES) if piece[0] == step] for step in MASKED_STEPS}
         look_up(0, 0, BANK)
         look_up(0, BANK, BANK)
-        smaller_on_vector(0, [0], 0, BANK)
-        smaller_on_vector(1, [0], BANK, T - SLIVER - BANK)
-        for i in of_step[1]:
+        smaller_on_vector(*project_for_vector(0, [0], 0, BANK))
+        fetch_y(0)
+        smaller_on_vector(*project_for_vector(1, [0], BANK, T - SLIVER - BANK))
+        last = project_for_vector(4, [0, 3], T - SLIVER, SLIVER)
+        step, first, width, bank = PIECES[0]
+        cols = slice(first, first + width)
+        first_gap = keep.tile([P, width], F32, name="first_gap")
+        nc.gpsimd.tensor_tensor(first_gap[:], old[:, ROW[step], cols], minus_y[step][:, cols], ALU.add)
+        nc.scalar.activation(signs[:, :width], first_gap[:], ACT.Sign)
+        masks_from(signs[:, :width], step, cols)
+        for i in of_step[1][1:]:
             fetch_y(i)
-        for i in of_step[1]:
+        for i in of_step[1][1:]:
             make_masks(i)
         for i in of_step[2]:
             fetch_y(i)
         look_up(2, 0, T)
         look_up(3, T - BANK // 2, BANK // 2)
         look_up(3, 0, BANK)
-        smaller_on_vector(4, [1, 0, 2, 3], T - SLIVER, SLIVER)
+        smaller_on_vector(*last)
         look_up(3, BANK, BANK // 2)
         for i in of_step[3]:
             fetch_y(i)
         for i in of_step[2] + of_step[3]:
             make_masks(i)
         products = keep.tile([P, 2, T], F32, name="products")
-        parts = [(1, slice(PIECES[i][1], PIECES[i][1] + PIECES[i][2])) for i in of_step[1]] + [(step, slice(0, T - SLIVER)) for step in MASKED_STEPS[1:]]
-        for step, part in parts:
-            nc.gpsimd.tensor_tensor(products[:, :, part], choice[step][:, :, part], old[:, ROW[step] : ROW[step] + PACK + 1 : PACK, part], ALU.mult)
-            nc.gpsimd.tensor_tensor(new[:, ROW[step], part], products[:, 0, part], products[:, 1, part], ALU.add)
+        for step, edges in ROUNDS:
+            for part in map(slice, edges[:-1], edges[1:]):
+                nc.gpsimd.tensor_tensor(products[:, :, part], choice[step][:, :, part], old[:, ROW[step] : ROW[step] + PACK + 1 : PACK, part], ALU.mult)
+            whole = slice(edges[0], edges[-1])
+            nc.gpsimd.tensor_tensor(new[:, ROW[step], whole], products[:, 0, whole], products[:, 1, whole], ALU.add)
 
         pairs = shared.tile([P, U, 2], BF16, name="pairs", align_bytes=64, offset=0)
         pair_words = pairs[:].rearrange("p c t -> p (c t)").bitcast(U32)

@@ -1,7 +1,6 @@
 from contextlib import ExitStack
 
 import concourse.mybir as mybir
-from concourse.masks import make_identity
 
 K, T, N, U = 512, 1024, 512, 2048
 FLOPS = 2 * K * N * T
@@ -23,19 +22,13 @@ BANK = 512
 LANES = 16
 QUADRANTS = 4
 GROUP = 512
+QUARTER = T // 4
 
-ORDER = (0, 1, 2, 3)
-MASKED_STEPS = (1, 2, 3)
-ROW = {1: 0, 0: 1, 3: 2, 2: 3}
-SLIVER = 128
-PIECES = ((1, 0, 256, 2), (1, 256, 384, 3), (1, 640, 384, 5), (2, 0, 512, 0), (2, 512, 512, 1), (3, 0, 512, 3), (3, 512, 384, 5))
-ROUNDS = ((1, (0, 256)), (1, (256, 640, T)), (2, (0, BANK, T)), (3, (0, T - SLIVER)))
 W_ON_SCALAR = 40
-POOL_FROM = 1536
-
-CHUNKS = [(0, 512, True), (512, 384, True), (896, 384, False), (1280, 256, False), (1536, 256, False), (1792, 256, False)]
-CALLS = [(0, 256), (256, 256), (512, 256), (768, 128), (896, 128), (1024, 256), (1280, 256), (1536, 256), (1792, 256)]
-WORD_STORES = [(0, 768), (768, 512), (1280, 512), (1792, 256)]
+SCALAR_PIECES = ((0, 256), (256, 384), (640, 384))
+PAIR_CHUNKS = ((0, 256), (256, 768), (1024, 1024))
+CHUNKS = [(0, 256, False), (256, 256, False), (512, 512, False), (1024, 256, True), (1280, 256, False), (1536, 256, False), (1792, 256, False)]
+WORD_STORES = [(0, 1024), (1024, 512), (1536, 256), (1792, 256)]
 
 
 def tile_picked_widxput_min_lo_kernel(tc, x_words, x_scales, mem, w1, slot, out_0, out_1, out_2):
@@ -46,177 +39,105 @@ def tile_picked_widxput_min_lo_kernel(tc, x_words, x_scales, mem, w1, slot, out_
 
     with ExitStack() as ctx:
         keep = ctx.enter_context(tc.tile_pool(name="keep", bufs=1))
-        shared = ctx.enter_context(tc.tile_pool(name="shared", bufs=1))
         psum = ctx.enter_context(tc.psum_pool(name="psum", bufs=1))
 
         offsets = keep.tile([P, T // LANES], U16, name="offsets")
-        store = [keep.tile([P, U], F32, name="store%d" % step) for step in range(PACK)]
-        old = keep.tile([P, 2 * PACK, T], F32, name="old")
+        store = [keep.tile([P, U], F32, name="store%d" % t) for t in range(PACK)]
+        old = keep.tile([P, PACK, T], F32, name="old")
         new = keep.tile([P, PACK, T], F32, name="new")
-        w_raw = old[:, ROW[0] : ROW[0] + 2, :].rearrange("p r (h c) -> p (r h) c", c=N)
+        w_raw = keep.tile([P, PACK, N], F32, name="w_raw")
         x_plane = keep.tile([P, T], U8, name="x_plane", align_bytes=64)
         x_codes = keep.tile([P, 2 * T], U8, name="x_codes", align_bytes=64)
         nc.vector.memset(x_plane[:].bitcast(I32), 0)
-        nc.sync.dma_start(store[1][:], mem_rows[:, ORDER[1], :])
+        nc.sync.dma_start(w_raw[:], w1.rearrange("(p j) c -> p j c", j=PACK))
         nc.sync.dma_start(offsets[:], slot)
-        nc.sync.dma_start(w_raw, w1.rearrange("(p j) c -> p j c", j=PACK))
-        nc.sync.dma_start(store[0][:], mem_rows[:, ORDER[0], :])
         nc.sync.dma_start(x_codes[:].bitcast(I32), x_words[0].bitcast(I32))
         for q in range(QUADRANTS):
             nc.sync.dma_start(x_plane[32 * q : 32 * q + 4, :].bitcast(I32), x_scales[0, 4 * q : 4 * q + 4, :].bitcast(I32))
-        for step in range(2, PACK):
-            nc.sync.dma_start(store[step][:], mem_rows[:, ORDER[step], :])
+        for t in range(PACK):
+            nc.sync.dma_start(store[t][:], mem_rows[:, t, :])
 
-        ident_f32 = keep.tile([P, P], F32, name="ident_f32")
-        ident_bf16 = keep.tile([P, P], BF16, name="ident_bf16")
-        make_identity(nc, ident_f32[:])
-        make_identity(nc, ident_bf16[:])
-
-        nc.vector.tensor_copy(old[:, ROW[1], :], store[1][:].indirect(offsets[:]))
-
-        w_by_m = w_raw.rearrange("p j (m t) -> p m t j", t=PACK)
+        w_by_m = w_raw[:].rearrange("p j (m t) -> p m t j", t=PACK)
         w_round = keep.tile([P, PACK, P, PACK], BF16, name="w_round", align_bytes=64)
         w_round_by_m = w_round[:].rearrange("p t m j -> p m t j")
-        all_codes = keep.tile([P, N], U32, name="w_codes", align_bytes=64)
-        all_planes = keep.tile([P, N], U8, name="w_plane", align_bytes=64)
-        w_codes = [all_codes[:, P * t : P * (t + 1)] for t in ORDER]
-        w_plane = [all_planes[:, P * t : P * (t + 1)] for t in ORDER]
+        w_codes = keep.tile([P, N], U32, name="w_codes", align_bytes=64)
+        w_plane = keep.tile([P, N], U8, name="w_plane", align_bytes=64)
         nc.scalar.copy(w_round_by_m[:, :W_ON_SCALAR], w_by_m[:, :W_ON_SCALAR])
         nc.vector.tensor_copy(w_round_by_m[:, W_ON_SCALAR:], w_by_m[:, W_ON_SCALAR:])
-        nc.vector.quantize_mx(out=all_codes[:].bitcast(FP8X4), scales=all_planes[:], in_=w_round[:].rearrange("p t m j -> p (t m j)"))
+        nc.vector.quantize_mx(out=w_codes[:].bitcast(FP8X4), scales=w_plane[:], in_=w_round[:].rearrange("p t m j -> p (t m j)"))
 
-        def project(out, step, first, width):
-            done = 0
-            for count in (BANK, BANK // 2, BANK // 4, BANK // 8):
-                if width - done >= count:
-                    start = first + done
-                    nc.tensor.matmul_mx(
-                        out=out[:, done : done + count],
-                        lhsT=w_codes[step].bitcast(FP8X4),
-                        lhsT_scale=w_plane[step],
-                        rhs=x_codes[:, 2 * start : 2 * (start + count)].bitcast(FP4X4),
-                        rhs_scale=x_plane[:, start : start + count],
-                        start=True,
-                        stop=True,
-                    )
-                    done = done + count
+        def project(out, t, first, width):
+            nc.tensor.matmul_mx(
+                out=out,
+                lhsT=w_codes[:, P * t : P * (t + 1)].bitcast(FP8X4),
+                lhsT_scale=w_plane[:, P * t : P * (t + 1)],
+                rhs=x_codes[:, 2 * first : 2 * (first + width)].bitcast(FP4X4),
+                rhs_scale=x_plane[:, first : first + width],
+                start=True,
+                stop=True,
+            )
 
-        def project_for_vector(bank, steps, first, width):
-            y = psum.tile([P, len(steps), width], F32, name="bank%d" % bank)
-            for i, step in enumerate(steps):
-                project(y[:, i, :], step, first, width)
-            return y, slice(ROW[steps[0]], ROW[steps[-1]] + 1), slice(first, first + width)
+        def entries(first, width):
+            return offsets[:, first // LANES : (first + width) // LANES]
 
-        def smaller_on_vector(y, rows, cols):
+        def look_up(t, first, width):
+            nc.vector.tensor_copy(old[:, t, first : first + width], store[t][:].indirect(entries(first, width)))
+
+        def smaller(bank, tiles, first, width):
+            y = psum.tile([P, len(tiles), width], F32, name="bank%d" % bank)
+            for i, t in enumerate(tiles):
+                project(y[:, i, :], t, first, width)
+            rows, cols = slice(tiles[0], tiles[-1] + 1), slice(first, first + width)
             nc.vector.tensor_tensor(new[:, rows, cols], old[:, rows, cols], y[:], ALU.min)
 
-        def look_up(step, first, width):
-            nc.vector.tensor_copy(old[:, ROW[step], first : first + width], store[step][:].indirect(offsets[:, first // LANES : (first + width) // LANES]))
+        def put_back_on_scalar(t):
+            for first, width in SCALAR_PIECES:
+                nc.scalar.activation(store[t][:].indirect(entries(first, width)), new[:, t, first : first + width], ACT.Copy)
+            nc.sync.dma_start(out_rows[:, t, :], store[t][:])
 
-
-        minus_y = {step: old[:, ROW[step] + PACK, :] for step in MASKED_STEPS}
-        choice = {step: keep.tile([P, 2, T], F32, name="choice%d" % step) for step in MASKED_STEPS}
-        keep_old = {step: choice[step][:, 0, :] for step in MASKED_STEPS}
-        take_new = {step: choice[step][:, 1, :] for step in MASKED_STEPS}
-        signs = shared.tile([P, U * 2], BF16, name="signs", align_bytes=64, offset=0)
-        minus_half = signs[:, 2 * U - 1 : 2 * U]
-        nc.vector.memset(minus_half, -0.5)
-
-        def fetch_y(i):
-            step, first, width, bank = PIECES[i]
-            y = psum.tile([P, width], F32, name="bank%d" % bank)
-            project(y[:], step, first, width)
-            nc.scalar.activation(minus_y[step][:, first : first + width], y[:], ACT.Copy, scale=-1.0)
-
-        def masks_from(sign, step, cols):
-            nc.scalar.activation(keep_old[step][:, cols], sign, ACT.Copy, scale=-0.5, bias=0.5)
-            nc.scalar.activation(take_new[step][:, cols], sign, ACT.Identity, scale=-0.5, bias=minus_half)
-
-        def make_masks(i):
-            step, first, width, bank = PIECES[i]
-            cols = slice(first, first + width)
-            gap = psum.tile([P, width], F32, name="bank%d" % bank)
-            for b in range(width // P):
-                block = slice(first + P * b, first + P * (b + 1))
-                nc.tensor.matmul(gap[:, P * b : P * (b + 1)], old[:, ROW[step], block], ident_f32[:], start=True, stop=False, is_transpose=True)
-                nc.tensor.matmul(gap[:, P * b : P * (b + 1)], minus_y[step][:, block], ident_f32[:], start=False, stop=True, is_transpose=True)
-            turned = signs[:, BANK * i : BANK * i + width]
-            nc.scalar.activation(turned, gap[:], ACT.Sign)
-            side = psum.tile([P, width], BF16, name="bank%d" % bank)
-            for b in range(width // P):
-                nc.tensor.transpose(side[:, P * b : P * (b + 1)], turned[:, P * b : P * (b + 1)], ident_bf16[:])
-            masks_from(side[:], step, cols)
-
-        of_step = {step: [i for i, piece in enumerate(PIECES) if piece[0] == step] for step in MASKED_STEPS}
-        look_up(0, 0, BANK)
-        look_up(0, BANK, BANK)
-        smaller_on_vector(*project_for_vector(0, [0], 0, BANK))
-        fetch_y(0)
-        smaller_on_vector(*project_for_vector(1, [0], BANK, T - SLIVER - BANK))
-        last = project_for_vector(4, [0, 3], T - SLIVER, SLIVER)
-        step, first, width, bank = PIECES[0]
-        cols = slice(first, first + width)
-        first_gap = keep.tile([P, width], F32, name="first_gap")
-        nc.gpsimd.tensor_tensor(first_gap[:], old[:, ROW[step], cols], minus_y[step][:, cols], ALU.add)
-        nc.scalar.activation(signs[:, :width], first_gap[:], ACT.Sign)
-        masks_from(signs[:, :width], step, cols)
-        for i in of_step[1][1:]:
-            fetch_y(i)
-        for i in of_step[1][1:]:
-            make_masks(i)
-        for i in of_step[2]:
-            fetch_y(i)
+        nc.scalar.activation(old[:, 0, :QUARTER], store[0][:].indirect(entries(0, QUARTER)), ACT.Copy)
+        look_up(0, QUARTER, T - QUARTER)
+        smaller(0, [0], 0, QUARTER)
+        smaller(1, [0], QUARTER, QUARTER)
+        smaller(2, [0], BANK, BANK)
+        put_back_on_scalar(0)
+        look_up(1, 0, T)
+        smaller(3, [1], 0, BANK)
+        smaller(4, [1], BANK, BANK)
+        put_back_on_scalar(1)
         look_up(2, 0, T)
-        look_up(3, T - BANK // 2, BANK // 2)
-        look_up(3, 0, BANK)
-        smaller_on_vector(*last)
-        look_up(3, BANK, BANK // 2)
-        for i in of_step[3]:
-            fetch_y(i)
-        for i in of_step[2] + of_step[3]:
-            make_masks(i)
-        products = keep.tile([P, 2, T], F32, name="products")
-        for step, edges in ROUNDS:
-            for part in map(slice, edges[:-1], edges[1:]):
-                nc.gpsimd.tensor_tensor(products[:, :, part], choice[step][:, :, part], old[:, ROW[step] : ROW[step] + PACK + 1 : PACK, part], ALU.mult)
-            whole = slice(edges[0], edges[-1])
-            nc.gpsimd.tensor_tensor(new[:, ROW[step], whole], products[:, 0, whole], products[:, 1, whole], ALU.add)
+        smaller(5, [2], 0, BANK)
+        look_up(3, 0, T)
+        smaller(6, [3], 0, BANK)
+        smaller(7, [2, 3], BANK, QUARTER)
+        smaller(0, [2, 3], BANK + QUARTER, QUARTER)
+        nc.vector.tensor_copy(store[2][:].indirect(offsets[:]), new[:, 2, :])
+        nc.sync.dma_start(out_rows[:, 2, :], store[2][:])
+        put_back_on_scalar(3)
 
-        pairs = shared.tile([P, U, 2], BF16, name="pairs", align_bytes=64, offset=0)
-        pair_words = pairs[:].rearrange("p c t -> p (c t)").bitcast(U32)
-        rounded = [keep.tile([P, width, PACK], BF16, name="rounded%d" % c, align_bytes=64) for c, (first, width, on_vector) in enumerate(CHUNKS)]
+        pairs = keep.tile([P, 2, U, 2], BF16, name="pairs", align_bytes=64)
+        for t in range(2):
+            nc.gpsimd.tensor_scalar(pairs[:, 0, :, t], store[t][:], 1.0, -0.0, ALU.mult, ALU.add)
+        nc.vector.tensor_copy(pairs[:, 1, :, 0], store[2][:])
+        for first, width in PAIR_CHUNKS:
+            nc.vector.tensor_copy(pairs[:, 1, first : first + width, 1], store[3][:, first : first + width])
         words = keep.tile([P, U], U32, name="words", align_bytes=64)
         plane = keep.tile([P, GROUP], U8, name="plane", align_bytes=64)
-
-        for step, t in enumerate(ORDER):
-            nc.vector.tensor_copy(store[step][:].indirect(offsets[:]), new[:, ROW[step], :])
-            nc.sync.dma_start(out_rows[:, t, :], store[step][:])
-            if step < 2:
-                nc.scalar.copy(pairs[:, :, t], store[step][:])
-            for c, (first, width, on_vector) in sorted(enumerate(CHUNKS), reverse=step == 1):
-                values = store[step][:, first : first + width]
-                both = values.unsqueeze(2).to_broadcast([P, width, 2])
-                on_pool = POOL_FROM <= first
-                if step == 1:
-                    as_words = rounded[c][:].rearrange("p c t -> p (c t)").bitcast(U32).rearrange("p (c u) -> p c u", u=2)
-                    nc.scalar.copy(as_words, pair_words[:, first : first + width].unsqueeze(2).to_broadcast([P, width, 2]))
-                elif step == 2 and on_pool:
-                    nc.gpsimd.tensor_scalar(rounded[c][:, :, 2:], both, 1.0, -0.0, ALU.mult, ALU.add)
-                elif step == 2 and on_vector:
-                    nc.scalar.copy(rounded[c][:, :, 2:], both)
-                elif step == 3 and on_vector:
-                    nc.vector.tensor_copy(rounded[c][:, :, t], values)
-                elif step >= 2:
-                    nc.scalar.copy(rounded[c][:, :, t], values)
-
-        for first, width in CALLS:
-            c = [i for i, chunk in enumerate(CHUNKS) if chunk[0] <= first < chunk[0] + chunk[1]][0]
-            inside = first - CHUNKS[c][0]
+        woven = [keep.tile([P, width, PACK], BF16, name="woven%d" % c, align_bytes=64) for c, (first, width, on_vector) in enumerate(CHUNKS)]
+        for c, (first, width, on_vector) in enumerate(CHUNKS):
+            view = I32 if on_vector else U32
+            source = pairs[:].rearrange("p h c e -> p h (c e)").bitcast(view)[:, :, first : first + width].rearrange("p h c -> p c h")
+            target = woven[c][:].rearrange("p c t -> p (c t)").bitcast(view).rearrange("p (c h) -> p c h", h=2)
+            if on_vector:
+                nc.vector.tensor_copy(target, source)
+            else:
+                nc.scalar.copy(target, source)
+        for c, (first, width, on_vector) in enumerate(CHUNKS):
             group, col = divmod(first, GROUP)
             nc.vector.quantize_mx(
                 out=words[:, first : first + width].bitcast(FP8X4),
                 scales=plane[4 * group :, col : col + width],
-                in_=rounded[c][:, inside : inside + width].rearrange("p c t -> p (c t)"),
+                in_=woven[c][:].rearrange("p c t -> p (c t)"),
             )
         for first, width in WORD_STORES:
             nc.sync.dma_start(out_words[:, first : first + width], words[:, first : first + width].bitcast(I32))

@@ -24,6 +24,7 @@ QUADRANTS = 4
 GROUP = 512
 QUARTER = T // 4
 
+ROW = (0, 1, 3, 2)
 W_ON_SCALAR = 40
 SCALAR_PIECES = ((0, 256), (256, 384), (640, 384))
 PAIR_CHUNKS = ((0, 256), (256, 768), (1024, 1024))
@@ -43,18 +44,20 @@ def tile_picked_widxput_min_lo_kernel(tc, x_words, x_scales, mem, w1, slot, out_
 
         offsets = keep.tile([P, T // LANES], U16, name="offsets")
         store = [keep.tile([P, U], F32, name="store%d" % t) for t in range(PACK)]
-        old = keep.tile([P, PACK, T], F32, name="old")
-        new = keep.tile([P, PACK, T], F32, name="new")
+        old = keep.tile([P, PACK * T], F32, name="old")
+        new = keep.tile([P, PACK * T], F32, name="new")
         w_raw = keep.tile([P, PACK, N], F32, name="w_raw")
         x_plane = keep.tile([P, T], U8, name="x_plane", align_bytes=64)
         x_codes = keep.tile([P, 2 * T], U8, name="x_codes", align_bytes=64)
         nc.vector.memset(x_plane[:].bitcast(I32), 0)
         nc.sync.dma_start(w_raw[:], w1.rearrange("(p j) c -> p j c", j=PACK))
         nc.sync.dma_start(offsets[:], slot)
-        nc.sync.dma_start(x_codes[:].bitcast(I32), x_words[0].bitcast(I32))
+        nc.sync.dma_start(store[0][:], mem_rows[:, 0, :])
         for q in range(QUADRANTS):
             nc.sync.dma_start(x_plane[32 * q : 32 * q + 4, :].bitcast(I32), x_scales[0, 4 * q : 4 * q + 4, :].bitcast(I32))
-        for t in range(PACK):
+        nc.sync.dma_start(x_codes[:, :BANK].bitcast(I32), x_words[0][:, :BANK].bitcast(I32))
+        nc.sync.dma_start(x_codes[:, BANK:].bitcast(I32), x_words[0][:, BANK:].bitcast(I32))
+        for t in range(1, PACK):
             nc.sync.dma_start(store[t][:], mem_rows[:, t, :])
 
         w_by_m = w_raw[:].rearrange("p j (m t) -> p m t j", t=PACK)
@@ -81,39 +84,51 @@ def tile_picked_widxput_min_lo_kernel(tc, x_words, x_scales, mem, w1, slot, out_
             return offsets[:, first // LANES : (first + width) // LANES]
 
         def look_up(t, first, width):
-            nc.vector.tensor_copy(old[:, t, first : first + width], store[t][:].indirect(entries(first, width)))
+            at = ROW[t] * T + first
+            nc.vector.tensor_copy(old[:, at : at + width], store[t][:].indirect(entries(first, width)))
 
-        def smaller(bank, tiles, first, width):
-            y = psum.tile([P, len(tiles), width], F32, name="bank%d" % bank)
-            for i, t in enumerate(tiles):
-                project(y[:, i, :], t, first, width)
-            rows, cols = slice(tiles[0], tiles[-1] + 1), slice(first, first + width)
-            nc.vector.tensor_tensor(new[:, rows, cols], old[:, rows, cols], y[:], ALU.min)
+        def smaller(bank, at, width):
+            y = psum.tile([P, width], F32, name="bank%d" % bank)
+            for done in range(0, width, QUARTER):
+                row, first = divmod(at + done, T)
+                project(y[:, done : done + QUARTER], ROW.index(row), first, QUARTER)
+            nc.vector.tensor_tensor(new[:, at : at + width], old[:, at : at + width], y[:], ALU.min)
 
-        def put_back_on_scalar(t):
-            for first, width in SCALAR_PIECES:
-                nc.scalar.activation(store[t][:].indirect(entries(first, width)), new[:, t, first : first + width], ACT.Copy)
-            nc.sync.dma_start(out_rows[:, t, :], store[t][:])
+        def put_back(t, piece):
+            first, width = SCALAR_PIECES[piece]
+            at = ROW[t] * T + first
+            nc.scalar.activation(store[t][:].indirect(entries(first, width)), new[:, at : at + width], ACT.Copy)
+            if piece == len(SCALAR_PIECES) - 1:
+                nc.sync.dma_start(out_rows[:, t, :], store[t][:])
 
-        nc.scalar.activation(old[:, 0, :QUARTER], store[0][:].indirect(entries(0, QUARTER)), ACT.Copy)
-        look_up(0, QUARTER, T - QUARTER)
-        smaller(0, [0], 0, QUARTER)
-        smaller(1, [0], QUARTER, QUARTER)
-        smaller(2, [0], BANK, BANK)
-        put_back_on_scalar(0)
-        look_up(1, 0, T)
-        smaller(3, [1], 0, BANK)
-        smaller(4, [1], BANK, BANK)
-        put_back_on_scalar(1)
-        look_up(2, 0, T)
-        smaller(5, [2], 0, BANK)
-        look_up(3, 0, T)
-        smaller(6, [3], 0, BANK)
-        smaller(7, [2, 3], BANK, QUARTER)
-        smaller(0, [2, 3], BANK + QUARTER, QUARTER)
-        nc.vector.tensor_copy(store[2][:].indirect(offsets[:]), new[:, 2, :])
+        look_up(0, 0, 384)
+        nc.scalar.activation(old[:, 384:T], store[0][:].indirect(entries(384, 640)), ACT.Copy)
+        smaller(0, 0, QUARTER)
+        smaller(1, QUARTER, BANK)
+        put_back(0, 0)
+        put_back(0, 1)
+        look_up(1, 0, BANK)
+        look_up(1, BANK, BANK)
+        smaller(2, T - QUARTER, BANK)
+        smaller(3, T + QUARTER, BANK)
+        put_back(1, 0)
+        put_back(0, 2)
+        put_back(1, 1)
+        look_up(2, 0, T - QUARTER)
+        look_up(2, T - QUARTER, QUARTER)
+        smaller(4, 3 * T + QUARTER, BANK)
+        smaller(0, 4 * T - QUARTER, QUARTER)
+        look_up(3, 0, T - QUARTER)
+        look_up(3, T - QUARTER, QUARTER)
+        smaller(5, 2 * T - QUARTER, BANK)
+        smaller(6, 3 * T - QUARTER, BANK)
+        smaller(7, 2 * T + QUARTER, BANK)
+        nc.vector.tensor_copy(store[2][:].indirect(offsets[:]), new[:, 3 * T :])
         nc.sync.dma_start(out_rows[:, 2, :], store[2][:])
-        put_back_on_scalar(3)
+        put_back(3, 0)
+        put_back(1, 2)
+        put_back(3, 1)
+        put_back(3, 2)
 
         pairs = keep.tile([P, 2, U, 2], BF16, name="pairs", align_bytes=64)
         for t in range(2):

@@ -24,9 +24,9 @@ QUADRANTS = 4
 GROUP = 512
 QUARTER = T // 4
 
-ROW = (0, 1, 3, 2)
+SCALAR_LOOKS = 256
 W_ON_SCALAR = 40
-SCALAR_PIECES = ((0, 256), (256, 384), (640, 384))
+SCALAR_PIECES = {0: ((0, 256), (256, 384), (640, 384)), 1: ((0, 384), (384, 384), (768, 256)), 3: ((0, 256), (256, 384), (640, 384))}
 PAIR_CHUNKS = ((0, 256), (256, 768), (1024, 1024))
 CHUNKS = [(0, 256, False), (256, 256, False), (512, 512, False), (1024, 256, True), (1280, 256, False), (1536, 256, False), (1792, 256, False)]
 WORD_STORES = [(0, 1024), (1024, 512), (1536, 256), (1792, 256)]
@@ -44,8 +44,8 @@ def tile_picked_widxput_min_lo_kernel(tc, x_words, x_scales, mem, w1, slot, out_
 
         offsets = keep.tile([P, T // LANES], U16, name="offsets")
         store = [keep.tile([P, U], F32, name="store%d" % t) for t in range(PACK)]
-        old = keep.tile([P, PACK * T], F32, name="old")
-        new = keep.tile([P, PACK * T], F32, name="new")
+        old = keep.tile([P, PACK, T], F32, name="old")
+        new = keep.tile([P, PACK, T], F32, name="new")
         w_raw = keep.tile([P, PACK, N], F32, name="w_raw")
         x_plane = keep.tile([P, T], U8, name="x_plane", align_bytes=64)
         x_codes = keep.tile([P, 2 * T], U8, name="x_codes", align_bytes=64)
@@ -84,49 +84,56 @@ def tile_picked_widxput_min_lo_kernel(tc, x_words, x_scales, mem, w1, slot, out_
             return offsets[:, first // LANES : (first + width) // LANES]
 
         def look_up(t, first, width):
-            at = ROW[t] * T + first
-            nc.vector.tensor_copy(old[:, at : at + width], store[t][:].indirect(entries(first, width)))
+            nc.vector.tensor_copy(old[:, t, first : first + width], store[t][:].indirect(entries(first, width)))
 
-        def smaller(bank, at, width):
-            y = psum.tile([P, width], F32, name="bank%d" % bank)
-            for done in range(0, width, QUARTER):
-                row, first = divmod(at + done, T)
-                project(y[:, done : done + QUARTER], ROW.index(row), first, QUARTER)
-            nc.vector.tensor_tensor(new[:, at : at + width], old[:, at : at + width], y[:], ALU.min)
+        def look_up_on_scalar(t, first, width):
+            nc.scalar.activation(old[:, t, first : first + width], store[t][:].indirect(entries(first, width)), ACT.Copy)
+
+        def quarters(tile, one, other):
+            flat = tile[:].rearrange("p t (q c) -> p (t q) c", c=QUARTER)
+            start, stop = PACK * one[0] + one[1], PACK * other[0] + other[1]
+            return flat[:, start : stop + 1 : max(stop - start, 1), :]
+
+        def smaller(bank, one, other):
+            parts = sorted({one, other})
+            y = psum.tile([P, len(parts), QUARTER], F32, name="bank%d" % bank)
+            for i, (t, quarter) in enumerate(parts):
+                project(y[:, i, :], t, quarter * QUARTER, QUARTER)
+            nc.vector.tensor_tensor(quarters(new, one, other), quarters(old, one, other), y[:], ALU.min)
 
         def put_back(t, piece):
-            first, width = SCALAR_PIECES[piece]
-            at = ROW[t] * T + first
-            nc.scalar.activation(store[t][:].indirect(entries(first, width)), new[:, at : at + width], ACT.Copy)
-            if piece == len(SCALAR_PIECES) - 1:
+            first, width = SCALAR_PIECES[t][piece]
+            nc.scalar.activation(store[t][:].indirect(entries(first, width)), new[:, t, first : first + width], ACT.Copy)
+            if first + width == T:
                 nc.sync.dma_start(out_rows[:, t, :], store[t][:])
 
         look_up(0, 0, 384)
-        nc.scalar.activation(old[:, 384:T], store[0][:].indirect(entries(384, 640)), ACT.Copy)
-        smaller(0, 0, QUARTER)
-        smaller(1, QUARTER, BANK)
+        look_up_on_scalar(0, 384, 640)
+        smaller(0, (0, 0), (0, 0))
+        smaller(1, (0, 1), (0, 2))
         put_back(0, 0)
         put_back(0, 1)
         look_up(1, 0, BANK)
         look_up(1, BANK, BANK)
-        smaller(2, T - QUARTER, BANK)
-        smaller(3, T + QUARTER, BANK)
+        smaller(2, (1, 0), (1, 1))
         put_back(1, 0)
+        look_up(2, 0, BANK)
+        look_up(2, BANK, BANK - SCALAR_LOOKS)
+        look_up_on_scalar(2, T - SCALAR_LOOKS, SCALAR_LOOKS)
+        smaller(3, (0, 3), (2, 0))
+        smaller(4, (1, 2), (2, 1))
         put_back(0, 2)
         put_back(1, 1)
-        look_up(2, 0, T - QUARTER)
-        look_up(2, T - QUARTER, QUARTER)
-        smaller(4, 3 * T + QUARTER, BANK)
-        smaller(0, 4 * T - QUARTER, QUARTER)
         look_up(3, 0, T - QUARTER)
         look_up(3, T - QUARTER, QUARTER)
-        smaller(5, 2 * T - QUARTER, BANK)
-        smaller(6, 3 * T - QUARTER, BANK)
-        smaller(7, 2 * T + QUARTER, BANK)
-        nc.vector.tensor_copy(store[2][:].indirect(offsets[:]), new[:, 3 * T :])
-        nc.sync.dma_start(out_rows[:, 2, :], store[2][:])
+        smaller(5, (1, 3), (3, 0))
+        smaller(6, (2, 3), (3, 3))
+        smaller(0, (2, 2), (2, 2))
+        smaller(7, (3, 1), (3, 2))
+        nc.vector.tensor_copy(store[2][:].indirect(offsets[:]), new[:, 2, :])
         put_back(3, 0)
         put_back(1, 2)
+        nc.sync.dma_start(out_rows[:, 2, :], store[2][:])
         put_back(3, 1)
         put_back(3, 2)
 

@@ -24,12 +24,11 @@ QUADRANTS = 4
 GROUP = 512
 QUARTER = T // 4
 
-SCALAR_LOOKS = 256
 W_ON_SCALAR = 40
-SCALAR_PIECES = {0: ((0, 256), (256, 384), (640, 384)), 1: ((0, 384), (384, 384), (768, 256)), 3: ((0, 256), (256, 384), (640, 384))}
-PAIR_CHUNKS = ((0, 256), (256, 768), (1024, 1024))
-CHUNKS = [(0, 256, False), (256, 256, False), (512, 512, False), (1024, 256, True), (1280, 256, False), (1536, 256, False), (1792, 256, False)]
-WORD_STORES = [(0, 1024), (1024, 512), (1536, 256), (1792, 256)]
+SCALAR_PIECES = ((0, 256), (256, 384), (640, 384))
+CHUNK = 256
+PAIR_CHUNKS = ((0, 256), (256, 768), (1024, 768))
+SCALAR_WEAVES = ((0, 256), (256, 256), (768, 256), (1024, 256), (1280, 256), (1536, 256), (1920, 128))
 
 
 def tile_picked_widxput_min_lo_kernel(tc, x_words, x_scales, mem, w1, slot, out_0, out_1, out_2):
@@ -56,8 +55,10 @@ def tile_picked_widxput_min_lo_kernel(tc, x_words, x_scales, mem, w1, slot, out_
         for q in range(QUADRANTS):
             nc.sync.dma_start(x_plane[32 * q : 32 * q + 4, :].bitcast(I32), x_scales[0, 4 * q : 4 * q + 4, :].bitcast(I32))
         nc.sync.dma_start(x_codes[:, :BANK].bitcast(I32), x_words[0][:, :BANK].bitcast(I32))
-        nc.sync.dma_start(x_codes[:, BANK:].bitcast(I32), x_words[0][:, BANK:].bitcast(I32))
-        for t in range(1, PACK):
+        nc.sync.dma_start(x_codes[:, BANK : 3 * BANK].bitcast(I32), x_words[0][:, BANK : 3 * BANK].bitcast(I32))
+        nc.sync.dma_start(store[1][:], mem_rows[:, 1, :])
+        nc.sync.dma_start(x_codes[:, 3 * BANK :].bitcast(I32), x_words[0][:, 3 * BANK :].bitcast(I32))
+        for t in range(2, PACK):
             nc.sync.dma_start(store[t][:], mem_rows[:, t, :])
 
         w_by_m = w_raw[:].rearrange("p j (m t) -> p m t j", t=PACK)
@@ -102,33 +103,33 @@ def tile_picked_widxput_min_lo_kernel(tc, x_words, x_scales, mem, w1, slot, out_
             nc.vector.tensor_tensor(quarters(new, one, other), quarters(old, one, other), y[:], ALU.min)
 
         def put_back(t, piece):
-            first, width = SCALAR_PIECES[t][piece]
+            first, width = SCALAR_PIECES[piece]
             nc.scalar.activation(store[t][:].indirect(entries(first, width)), new[:, t, first : first + width], ACT.Copy)
             if first + width == T:
                 nc.sync.dma_start(out_rows[:, t, :], store[t][:])
 
-        look_up(0, 0, 384)
-        look_up_on_scalar(0, 384, 640)
+        look_up(0, 0, QUARTER)
+        look_up(0, QUARTER, 224)
+        look_up_on_scalar(0, 480, 544)
         smaller(0, (0, 0), (0, 0))
         smaller(1, (0, 1), (0, 2))
         put_back(0, 0)
         put_back(0, 1)
         look_up(1, 0, BANK)
         look_up(1, BANK, BANK)
-        smaller(2, (1, 0), (1, 1))
+        smaller(0, (1, 0), (1, 0))
+        smaller(2, (0, 3), (1, 1))
         put_back(1, 0)
-        look_up(2, 0, BANK)
-        look_up(2, BANK, BANK - SCALAR_LOOKS)
-        look_up_on_scalar(2, T - SCALAR_LOOKS, SCALAR_LOOKS)
-        smaller(3, (0, 3), (2, 0))
-        smaller(4, (1, 2), (2, 1))
         put_back(0, 2)
+        look_up(2, 0, T - QUARTER)
+        look_up(2, T - QUARTER, QUARTER)
+        smaller(3, (1, 2), (2, 0))
+        smaller(4, (2, 1), (2, 2))
         put_back(1, 1)
         look_up(3, 0, T - QUARTER)
         look_up(3, T - QUARTER, QUARTER)
         smaller(5, (1, 3), (3, 0))
         smaller(6, (2, 3), (3, 3))
-        smaller(0, (2, 2), (2, 2))
         smaller(7, (3, 1), (3, 2))
         nc.vector.tensor_copy(store[2][:].indirect(offsets[:]), new[:, 2, :])
         put_back(3, 0)
@@ -140,29 +141,52 @@ def tile_picked_widxput_min_lo_kernel(tc, x_words, x_scales, mem, w1, slot, out_
         pairs = keep.tile([P, 2, U, 2], BF16, name="pairs", align_bytes=64)
         for t in range(2):
             nc.gpsimd.tensor_scalar(pairs[:, 0, :, t], store[t][:], 1.0, -0.0, ALU.mult, ALU.add)
-        nc.vector.tensor_copy(pairs[:, 1, :, 0], store[2][:])
+        own = slice(U - CHUNK, U)
+        nc.vector.tensor_copy(pairs[:, 1, : U - CHUNK, 0], store[2][:, : U - CHUNK])
+        nc.vector.tensor_copy(pairs[:, 1, own, :], store[2][:, own].unsqueeze(2).to_broadcast([P, CHUNK, 2]))
+        nc.scalar.copy(pairs[:, 1, own, 1], store[3][:, own])
         for first, width in PAIR_CHUNKS:
             nc.vector.tensor_copy(pairs[:, 1, first : first + width, 1], store[3][:, first : first + width])
         words = keep.tile([P, U], U32, name="words", align_bytes=64)
         plane = keep.tile([P, GROUP], U8, name="plane", align_bytes=64)
-        woven = [keep.tile([P, width, PACK], BF16, name="woven%d" % c, align_bytes=64) for c, (first, width, on_vector) in enumerate(CHUNKS)]
-        for c, (first, width, on_vector) in enumerate(CHUNKS):
+        woven = keep.tile([P, U, PACK], BF16, name="woven", align_bytes=64)
+
+        def weave(first, width, on_vector):
             view = I32 if on_vector else U32
             source = pairs[:].rearrange("p h c e -> p h (c e)").bitcast(view)[:, :, first : first + width].rearrange("p h c -> p c h")
-            target = woven[c][:].rearrange("p c t -> p (c t)").bitcast(view).rearrange("p (c h) -> p c h", h=2)
+            target = woven[:, first : first + width].rearrange("p c t -> p (c t)").bitcast(view).rearrange("p (c h) -> p c h", h=2)
             if on_vector:
                 nc.vector.tensor_copy(target, source)
             else:
                 nc.scalar.copy(target, source)
-        for c, (first, width, on_vector) in enumerate(CHUNKS):
+
+        def quantise(first, width):
             group, col = divmod(first, GROUP)
             nc.vector.quantize_mx(
                 out=words[:, first : first + width].bitcast(FP8X4),
                 scales=plane[4 * group :, col : col + width],
-                in_=woven[c][:].rearrange("p c t -> p (c t)"),
+                in_=woven[:, first : first + width].rearrange("p c t -> p (c t)"),
             )
-        for first, width in WORD_STORES:
+
+        def store_words(first, width):
             nc.sync.dma_start(out_words[:, first : first + width], words[:, first : first + width].bitcast(I32))
+
+        for first, width in SCALAR_WEAVES:
+            weave(first, width, False)
+        quantise(0, 256)
+        weave(512, 256, True)
+        quantise(256, 256)
+        weave(1792, 128, True)
+        quantise(512, 256)
+        store_words(0, 768)
+        quantise(768, 256)
+        quantise(1024, 256)
+        quantise(1280, 256)
+        store_words(768, 768)
+        quantise(1792, 128)
+        quantise(1536, 256)
+        quantise(1920, 128)
+        store_words(1536, 512)
         for q in range(QUADRANTS):
             nc.scalar.dma_start(
                 out_2[0, 4 * q : 4 * q + 4, :].bitcast(I32).rearrange("r (g c) -> g r c", g=U // GROUP),

@@ -25,7 +25,8 @@ GROUP = 512
 QUARTER = T // 4
 
 W_ON_SCALAR = 40
-SCALAR_PIECES = ((0, 256), (256, 384), (640, 384))
+FIRST_ON_VECTOR = 480
+EARLY = 448
 CHUNK = 256
 PAIR_CHUNKS = ((0, 256), (256, 768), (1024, 768))
 SCALAR_WEAVES = ((0, 256), (256, 256), (768, 256), (1024, 256), (1280, 256), (1536, 256), (1920, 128))
@@ -57,9 +58,9 @@ def tile_picked_widxput_min_lo_kernel(tc, x_words, x_scales, mem, w1, slot, out_
         nc.sync.dma_start(x_codes[:, :BANK].bitcast(I32), x_words[0][:, :BANK].bitcast(I32))
         nc.sync.dma_start(x_codes[:, BANK : 3 * BANK].bitcast(I32), x_words[0][:, BANK : 3 * BANK].bitcast(I32))
         nc.sync.dma_start(store[1][:], mem_rows[:, 1, :])
-        nc.sync.dma_start(x_codes[:, 3 * BANK :].bitcast(I32), x_words[0][:, 3 * BANK :].bitcast(I32))
         for t in range(2, PACK):
             nc.sync.dma_start(store[t][:], mem_rows[:, t, :])
+        nc.sync.dma_start(x_codes[:, 3 * BANK :].bitcast(I32), x_words[0][:, 3 * BANK :].bitcast(I32))
 
         w_by_m = w_raw[:].rearrange("p j (m t) -> p m t j", t=PACK)
         w_round = keep.tile([P, PACK, P, PACK], BF16, name="w_round", align_bytes=64)
@@ -102,41 +103,46 @@ def tile_picked_widxput_min_lo_kernel(tc, x_words, x_scales, mem, w1, slot, out_
                 project(y[:, i, :], t, quarter * QUARTER, QUARTER)
             nc.vector.tensor_tensor(quarters(new, one, other), quarters(old, one, other), y[:], ALU.min)
 
-        def put_back(t, piece):
-            first, width = SCALAR_PIECES[piece]
+        def put_back(t, first, width):
+            nc.vector.tensor_copy(store[t][:].indirect(entries(first, width)), new[:, t, first : first + width])
+
+        def put_back_on_scalar(t, first, width):
             nc.scalar.activation(store[t][:].indirect(entries(first, width)), new[:, t, first : first + width], ACT.Copy)
-            if first + width == T:
-                nc.sync.dma_start(out_rows[:, t, :], store[t][:])
+
+        def hand_out(t):
+            nc.sync.dma_start(out_rows[:, t, :], store[t][:])
 
         look_up(0, 0, QUARTER)
-        look_up(0, QUARTER, 224)
-        look_up_on_scalar(0, 480, 544)
+        look_up(0, QUARTER, FIRST_ON_VECTOR - QUARTER)
+        look_up_on_scalar(0, FIRST_ON_VECTOR, T - FIRST_ON_VECTOR)
         smaller(0, (0, 0), (0, 0))
         smaller(1, (0, 1), (0, 2))
-        put_back(0, 0)
-        put_back(0, 1)
+        put_back_on_scalar(0, 0, 256)
+        put_back_on_scalar(0, 256, 384)
         look_up(1, 0, BANK)
         look_up(1, BANK, BANK)
-        smaller(0, (1, 0), (1, 0))
-        smaller(2, (0, 3), (1, 1))
-        put_back(1, 0)
-        put_back(0, 2)
-        look_up(2, 0, T - QUARTER)
-        look_up(2, T - QUARTER, QUARTER)
-        smaller(3, (1, 2), (2, 0))
-        smaller(4, (2, 1), (2, 2))
-        put_back(1, 1)
-        look_up(3, 0, T - QUARTER)
-        look_up(3, T - QUARTER, QUARTER)
-        smaller(5, (1, 3), (3, 0))
-        smaller(6, (2, 3), (3, 3))
-        smaller(7, (3, 1), (3, 2))
-        nc.vector.tensor_copy(store[2][:].indirect(offsets[:]), new[:, 2, :])
-        put_back(3, 0)
-        put_back(1, 2)
-        nc.sync.dma_start(out_rows[:, 2, :], store[2][:])
-        put_back(3, 1)
-        put_back(3, 2)
+        smaller(2, (1, 0), (1, 1))
+        smaller(0, (1, 2), (1, 2))
+        put_back(1, 0, EARLY)
+        look_up_on_scalar(2, 0, T)
+        look_up_on_scalar(3, 0, T)
+        smaller(3, (2, 0), (2, 1))
+        smaller(4, (2, 2), (2, 3))
+        smaller(5, (0, 3), (1, 3))
+        put_back_on_scalar(0, 640, 384)
+        hand_out(0)
+        put_back(2, T - QUARTER, QUARTER)
+        smaller(6, (3, 0), (3, 1))
+        put_back(1, EARLY + QUARTER, T - QUARTER - EARLY)
+        smaller(7, (3, 2), (3, 3))
+        put_back_on_scalar(3, 0, 256)
+        put_back_on_scalar(1, EARLY, QUARTER)
+        hand_out(1)
+        put_back(2, 0, T - QUARTER)
+        hand_out(2)
+        put_back_on_scalar(3, 256, 384)
+        put_back_on_scalar(3, 640, 384)
+        hand_out(3)
 
         pairs = keep.tile([P, 2, U, 2], BF16, name="pairs", align_bytes=64)
         for t in range(2):

@@ -26,10 +26,10 @@ QUARTER = T // 4
 
 W_ON_SCALAR = 40
 FIRST_ON_VECTOR = 480
-EARLY = 448
-CHUNK = 256
-PAIR_CHUNKS = ((0, 256), (256, 768), (1024, 768))
-SCALAR_WEAVES = ((0, 256), (256, 256), (768, 256), (1024, 256), (1280, 256), (1536, 256), (1920, 128))
+SLIVER = 64
+OWN = 192
+PAIR_CHUNKS = ((0, 256), (256, 768), (1024, 1024 - OWN))
+SCALAR_WEAVES = ((0, 256), (256, 256), (896, 384), (1280, 256), (1536, 256), (1792, 128), (1920, 128))
 
 
 def tile_picked_widxput_min_lo_kernel(tc, x_words, x_scales, mem, w1, slot, out_0, out_1, out_2):
@@ -45,7 +45,8 @@ def tile_picked_widxput_min_lo_kernel(tc, x_words, x_scales, mem, w1, slot, out_
         offsets = keep.tile([P, T // LANES], U16, name="offsets")
         store = [keep.tile([P, U], F32, name="store%d" % t) for t in range(PACK)]
         old = keep.tile([P, PACK, T], F32, name="old")
-        new = keep.tile([P, PACK, T], F32, name="new")
+        shared = keep.tile([P, 2 * U - OWN - QUARTER + PACK * T], F32, name="shared", align_bytes=64)
+        new = shared[:, 2 * U - OWN - QUARTER :].rearrange("p (t c) -> p t c", t=PACK)
         w_raw = keep.tile([P, PACK, N], F32, name="w_raw")
         x_plane = keep.tile([P, T], U8, name="x_plane", align_bytes=64)
         x_codes = keep.tile([P, 2 * T], U8, name="x_codes", align_bytes=64)
@@ -58,9 +59,11 @@ def tile_picked_widxput_min_lo_kernel(tc, x_words, x_scales, mem, w1, slot, out_
         nc.sync.dma_start(x_codes[:, :BANK].bitcast(I32), x_words[0][:, :BANK].bitcast(I32))
         nc.sync.dma_start(x_codes[:, BANK : 3 * BANK].bitcast(I32), x_words[0][:, BANK : 3 * BANK].bitcast(I32))
         nc.sync.dma_start(store[1][:], mem_rows[:, 1, :])
+        nc.sync.dma_start(x_codes[:, 3 * BANK :].bitcast(I32), x_words[0][:, 3 * BANK :].bitcast(I32))
         for t in range(2, PACK):
             nc.sync.dma_start(store[t][:], mem_rows[:, t, :])
-        nc.sync.dma_start(x_codes[:, 3 * BANK :].bitcast(I32), x_words[0][:, 3 * BANK :].bitcast(I32))
+        nothing = keep.tile([P, SLIVER], F32, name="nothing")
+        nc.gpsimd.memset(nothing[:], -0.0)
 
         w_by_m = w_raw[:].rearrange("p j (m t) -> p m t j", t=PACK)
         w_round = keep.tile([P, PACK, P, PACK], BF16, name="w_round", align_bytes=64)
@@ -85,29 +88,32 @@ def tile_picked_widxput_min_lo_kernel(tc, x_words, x_scales, mem, w1, slot, out_
         def entries(first, width):
             return offsets[:, first // LANES : (first + width) // LANES]
 
+        def row(t):
+            return (t + 1) % PACK
+
         def look_up(t, first, width):
-            nc.vector.tensor_copy(old[:, t, first : first + width], store[t][:].indirect(entries(first, width)))
+            nc.vector.tensor_copy(old[:, row(t), first : first + width], store[t][:].indirect(entries(first, width)))
 
         def look_up_on_scalar(t, first, width):
-            nc.scalar.activation(old[:, t, first : first + width], store[t][:].indirect(entries(first, width)), ACT.Copy)
+            nc.scalar.activation(old[:, row(t), first : first + width], store[t][:].indirect(entries(first, width)), ACT.Copy)
 
-        def quarters(tile, one, other):
-            flat = tile[:].rearrange("p t (q c) -> p (t q) c", c=QUARTER)
-            start, stop = PACK * one[0] + one[1], PACK * other[0] + other[1]
+        def quarters(rows, parts):
+            flat = rows.rearrange("p t (q c) -> p (t q) c", c=QUARTER)
+            start, stop = (PACK * row(t) + quarter for t, quarter in (parts[0], parts[-1]))
             return flat[:, start : stop + 1 : max(stop - start, 1), :]
 
         def smaller(bank, one, other):
-            parts = sorted({one, other})
+            parts = sorted({one, other}, key=lambda part: (row(part[0]), part[1]))
             y = psum.tile([P, len(parts), QUARTER], F32, name="bank%d" % bank)
             for i, (t, quarter) in enumerate(parts):
                 project(y[:, i, :], t, quarter * QUARTER, QUARTER)
-            nc.vector.tensor_tensor(quarters(new, one, other), quarters(old, one, other), y[:], ALU.min)
+            nc.vector.tensor_tensor(quarters(new, parts), quarters(old[:], parts), y[:], ALU.min)
 
         def put_back(t, first, width):
-            nc.vector.tensor_copy(store[t][:].indirect(entries(first, width)), new[:, t, first : first + width])
+            nc.vector.tensor_copy(store[t][:].indirect(entries(first, width)), new[:, row(t), first : first + width])
 
         def put_back_on_scalar(t, first, width):
-            nc.scalar.activation(store[t][:].indirect(entries(first, width)), new[:, t, first : first + width], ACT.Copy)
+            nc.scalar.activation(store[t][:].indirect(entries(first, width)), new[:, row(t), first : first + width], ACT.Copy)
 
         def hand_out(t):
             nc.sync.dma_start(out_rows[:, t, :], store[t][:])
@@ -121,35 +127,38 @@ def tile_picked_widxput_min_lo_kernel(tc, x_words, x_scales, mem, w1, slot, out_
         put_back_on_scalar(0, 256, 384)
         look_up(1, 0, BANK)
         look_up(1, BANK, BANK)
-        smaller(2, (1, 0), (1, 1))
-        smaller(0, (1, 2), (1, 2))
-        put_back(1, 0, EARLY)
-        look_up_on_scalar(2, 0, T)
-        look_up_on_scalar(3, 0, T)
-        smaller(3, (2, 0), (2, 1))
-        smaller(4, (2, 2), (2, 3))
-        smaller(5, (0, 3), (1, 3))
+        smaller(0, (1, 0), (1, 0))
+        smaller(2, (0, 3), (1, 1))
+        put_back_on_scalar(1, 0, 256)
         put_back_on_scalar(0, 640, 384)
         hand_out(0)
-        put_back(2, T - QUARTER, QUARTER)
-        smaller(6, (3, 0), (3, 1))
-        put_back(1, EARLY + QUARTER, T - QUARTER - EARLY)
-        smaller(7, (3, 2), (3, 3))
+        look_up(2, 0, T - QUARTER)
+        look_up(2, T - QUARTER, QUARTER)
+        smaller(3, (1, 2), (2, 0))
+        smaller(4, (2, 1), (2, 2))
+        nc.vector.tensor_tensor(store[1][:].indirect(entries(640, SLIVER)), new[:, row(1), 640 : 640 + SLIVER], nothing[:], ALU.add)
+        put_back_on_scalar(1, 256, 384)
+        look_up(3, 0, T - QUARTER)
+        look_up(3, T - QUARTER, QUARTER)
+        smaller(5, (1, 3), (3, 0))
+        smaller(6, (2, 3), (3, 3))
+        smaller(7, (3, 1), (3, 2))
+        put_back(2, 0, T)
         put_back_on_scalar(3, 0, 256)
-        put_back_on_scalar(1, EARLY, QUARTER)
+        put_back_on_scalar(1, 640 + SLIVER, 384 - SLIVER)
         hand_out(1)
-        put_back(2, 0, T - QUARTER)
         hand_out(2)
         put_back_on_scalar(3, 256, 384)
         put_back_on_scalar(3, 640, 384)
         hand_out(3)
 
-        pairs = keep.tile([P, 2, U, 2], BF16, name="pairs", align_bytes=64)
+        pair_words = shared[:, : 2 * U]
+        pairs = pair_words.bitcast(BF16).rearrange("p (h c e) -> p h c e", h=2, e=2)
         for t in range(2):
             nc.gpsimd.tensor_scalar(pairs[:, 0, :, t], store[t][:], 1.0, -0.0, ALU.mult, ALU.add)
-        own = slice(U - CHUNK, U)
-        nc.vector.tensor_copy(pairs[:, 1, : U - CHUNK, 0], store[2][:, : U - CHUNK])
-        nc.vector.tensor_copy(pairs[:, 1, own, :], store[2][:, own].unsqueeze(2).to_broadcast([P, CHUNK, 2]))
+        own = slice(U - OWN, U)
+        nc.vector.tensor_copy(pairs[:, 1, : U - OWN, 0], store[2][:, : U - OWN])
+        nc.scalar.copy(pairs[:, 1, own, 0], store[2][:, own])
         nc.scalar.copy(pairs[:, 1, own, 1], store[3][:, own])
         for first, width in PAIR_CHUNKS:
             nc.vector.tensor_copy(pairs[:, 1, first : first + width, 1], store[3][:, first : first + width])
@@ -159,7 +168,7 @@ def tile_picked_widxput_min_lo_kernel(tc, x_words, x_scales, mem, w1, slot, out_
 
         def weave(first, width, on_vector):
             view = I32 if on_vector else U32
-            source = pairs[:].rearrange("p h c e -> p h (c e)").bitcast(view)[:, :, first : first + width].rearrange("p h c -> p c h")
+            source = pair_words.bitcast(view).rearrange("p (h c) -> p c h", h=2)[:, first : first + width, :]
             target = woven[:, first : first + width].rearrange("p c t -> p (c t)").bitcast(view).rearrange("p (c h) -> p c h", h=2)
             if on_vector:
                 nc.vector.tensor_copy(target, source)
@@ -179,18 +188,17 @@ def tile_picked_widxput_min_lo_kernel(tc, x_words, x_scales, mem, w1, slot, out_
 
         for first, width in SCALAR_WEAVES:
             weave(first, width, False)
+        weave(512, 384, True)
         quantise(0, 256)
-        weave(512, 256, True)
         quantise(256, 256)
-        weave(1792, 128, True)
         quantise(512, 256)
         store_words(0, 768)
         quantise(768, 256)
         quantise(1024, 256)
         quantise(1280, 256)
         store_words(768, 768)
-        quantise(1792, 128)
         quantise(1536, 256)
+        quantise(1792, 128)
         quantise(1920, 128)
         store_words(1536, 512)
         for q in range(QUADRANTS):

@@ -27,9 +27,9 @@ QUARTER = T // 4
 W_ON_SCALAR = 40
 FIRST_ON_VECTOR = 480
 SLIVER = 64
-OWN = 192
+OWN = 256
 PAIR_CHUNKS = ((0, 256), (256, 768), (1024, 1024 - OWN))
-SCALAR_WEAVES = ((0, 256), (256, 256), (896, 384), (1280, 256), (1536, 256), (1792, 128), (1920, 128))
+SCALAR_WEAVES = ((0, 256), (256, 256), (896, 384), (1280, 256), (1536, 256))
 
 
 def tile_picked_widxput_min_lo_kernel(tc, x_words, x_scales, mem, w1, slot, out_0, out_1, out_2):
@@ -127,22 +127,22 @@ def tile_picked_widxput_min_lo_kernel(tc, x_words, x_scales, mem, w1, slot, out_
         put_back_on_scalar(0, 256, 384)
         look_up(1, 0, BANK)
         look_up(1, BANK, BANK)
-        smaller(0, (1, 0), (1, 0))
-        smaller(2, (0, 3), (1, 1))
+        smaller(2, (0, 3), (1, 0))
         put_back_on_scalar(1, 0, 256)
         put_back_on_scalar(0, 640, 384)
         hand_out(0)
         look_up(2, 0, T - QUARTER)
         look_up(2, T - QUARTER, QUARTER)
         smaller(3, (1, 2), (2, 0))
-        smaller(4, (2, 1), (2, 2))
+        smaller(4, (1, 1), (2, 1))
         nc.vector.tensor_tensor(store[1][:].indirect(entries(640, SLIVER)), new[:, row(1), 640 : 640 + SLIVER], nothing[:], ALU.add)
         put_back_on_scalar(1, 256, 384)
         look_up(3, 0, T - QUARTER)
         look_up(3, T - QUARTER, QUARTER)
         smaller(5, (1, 3), (3, 0))
-        smaller(6, (2, 3), (3, 3))
-        smaller(7, (3, 1), (3, 2))
+        smaller(6, (2, 2), (3, 1))
+        smaller(7, (2, 3), (3, 2))
+        smaller(0, (3, 3), (3, 3))
         put_back(2, 0, T)
         put_back_on_scalar(3, 0, 256)
         put_back_on_scalar(1, 640 + SLIVER, 384 - SLIVER)
@@ -164,12 +164,15 @@ def tile_picked_widxput_min_lo_kernel(tc, x_words, x_scales, mem, w1, slot, out_
             nc.vector.tensor_copy(pairs[:, 1, first : first + width, 1], store[3][:, first : first + width])
         words = keep.tile([P, U], U32, name="words", align_bytes=64)
         plane = keep.tile([P, GROUP], U8, name="plane", align_bytes=64)
-        woven = keep.tile([P, U, PACK], BF16, name="woven", align_bytes=64)
+        woven = keep.tile([P, U - OWN, PACK], BF16, name="woven", align_bytes=64)
+
+        def room(first):
+            return first % (U - OWN)
 
         def weave(first, width, on_vector):
             view = I32 if on_vector else U32
             source = pair_words.bitcast(view).rearrange("p (h c) -> p c h", h=2)[:, first : first + width, :]
-            target = woven[:, first : first + width].rearrange("p c t -> p (c t)").bitcast(view).rearrange("p (c h) -> p c h", h=2)
+            target = woven[:, room(first) : room(first) + width].rearrange("p c t -> p (c t)").bitcast(view).rearrange("p (c h) -> p c h", h=2)
             if on_vector:
                 nc.vector.tensor_copy(target, source)
             else:
@@ -180,7 +183,7 @@ def tile_picked_widxput_min_lo_kernel(tc, x_words, x_scales, mem, w1, slot, out_
             nc.vector.quantize_mx(
                 out=words[:, first : first + width].bitcast(FP8X4),
                 scales=plane[4 * group :, col : col + width],
-                in_=woven[:, first : first + width].rearrange("p c t -> p (c t)"),
+                in_=woven[:, room(first) : room(first) + width].rearrange("p c t -> p (c t)"),
             )
 
         def store_words(first, width):
@@ -193,6 +196,8 @@ def tile_picked_widxput_min_lo_kernel(tc, x_words, x_scales, mem, w1, slot, out_
         quantise(256, 256)
         quantise(512, 256)
         store_words(0, 768)
+        weave(1792, 128, False)
+        weave(1920, 128, False)
         quantise(768, 256)
         quantise(1024, 256)
         quantise(1280, 256)

from contextlib import ExitStack

import concourse.mybir as mybir

K, T, N, U = 512, 1024, 512, 2048
FLOPS = 2 * K * N * T

F32 = mybir.dt.float32
BF16 = mybir.dt.bfloat16
I32 = mybir.dt.int32
U32 = mybir.dt.uint32
U16 = mybir.dt.uint16
U8 = mybir.dt.uint8
FP8X4 = mybir.dt.float8_e4m3fn_x4
FP4X4 = mybir.dt.float4_e2m1fn_x4
ALU = mybir.AluOpType
ACT = mybir.ActivationFunctionType

P = 128
PACK = 4
BANK = 512
LANES = 16
QUADRANTS = 4
GROUP = 512
QUARTER = T // 4

W_ON_SCALAR = 40
FIRST_ON_VECTOR = 480
SLIVER = 64
OWN = 256
PAIR_CHUNKS = ((0, 256), (256, 768), (1024, 1024 - OWN))
SCALAR_WEAVES = ((0, 256), (256, 256), (896, 384), (1280, 256), (1536, 256))


def tile_picked_widxput_min_lo_kernel(tc, x_words, x_scales, mem, w1, slot, out_0, out_1, out_2):
    nc = tc.nc
    mem_rows = mem.rearrange("(p t) c -> p t c", t=PACK)
    out_rows = out_0.rearrange("(p t) c -> p t c", t=PACK)
    out_words = out_1[0].rearrange("p c r -> p (c r)").bitcast(I32)

    with ExitStack() as ctx:
        keep = ctx.enter_context(tc.tile_pool(name="keep", bufs=1))
        psum = ctx.enter_context(tc.psum_pool(name="psum", bufs=1))

        offsets = keep.tile([P, T // LANES], U16, name="offsets")
        store = [keep.tile([P, U], F32, name="store%d" % t) for t in range(PACK)]
        old = keep.tile([P, PACK, T], F32, name="old")
        shared = keep.tile([P, 2 * U - OWN - QUARTER + PACK * T], F32, name="shared", align_bytes=64)
        new = shared[:, 2 * U - OWN - QUARTER :].rearrange("p (t c) -> p t c", t=PACK)
        w_raw = keep.tile([P, PACK, N], F32, name="w_raw")
        x_plane = keep.tile([P, T], U8, name="x_plane", align_bytes=64)
        x_codes = keep.tile([P, 2 * T], U8, name="x_codes", align_bytes=64)
        nc.vector.memset(x_plane[:].bitcast(I32), 0)
        nc.sync.dma_start(w_raw[:], w1.rearrange("(p j) c -> p j c", j=PACK))
        nc.sync.dma_start(offsets[:], slot)
        nc.sync.dma_start(store[0][:], mem_rows[:, 0, :])
        for q in range(QUADRANTS):
            nc.sync.dma_start(x_plane[32 * q : 32 * q + 4, :].bitcast(I32), x_scales[0, 4 * q : 4 * q + 4, :].bitcast(I32))
        nc.sync.dma_start(x_codes[:, :BANK].bitcast(I32), x_words[0][:, :BANK].bitcast(I32))
        nc.sync.dma_start(x_codes[:, BANK : 3 * BANK].bitcast(I32), x_words[0][:, BANK : 3 * BANK].bitcast(I32))
        nc.sync.dma_start(store[1][:], mem_rows[:, 1, :])
        nc.sync.dma_start(x_codes[:, 3 * BANK :].bitcast(I32), x_words[0][:, 3 * BANK :].bitcast(I32))
        for t in range(2, PACK):
            nc.sync.dma_start(store[t][:], mem_rows[:, t, :])
        nothing = keep.tile([P, SLIVER], F32, name="nothing")
        nc.gpsimd.memset(nothing[:], -0.0)

        w_by_m = w_raw[:].rearrange("p j (m t) -> p m t j", t=PACK)
        w_round = keep.tile([P, PACK, P, PACK], BF16, name="w_round", align_bytes=64)
        w_round_by_m = w_round[:].rearrange("p t m j -> p m t j")
        w_codes = keep.tile([P, N], U32, name="w_codes", align_bytes=64)
        w_plane = keep.tile([P, N], U8, name="w_plane", align_bytes=64)
        nc.scalar.copy(w_round_by_m[:, :W_ON_SCALAR], w_by_m[:, :W_ON_SCALAR])
        nc.vector.tensor_copy(w_round_by_m[:, W_ON_SCALAR:], w_by_m[:, W_ON_SCALAR:])
        nc.vector.quantize_mx(out=w_codes[:].bitcast(FP8X4), scales=w_plane[:], in_=w_round[:].rearrange("p t m j -> p (t m j)"))

        def project(out, t, first, width):
            nc.tensor.matmul_mx(
                out=out,
                lhsT=w_codes[:, P * t : P * (t + 1)].bitcast(FP8X4),
                lhsT_scale=w_plane[:, P * t : P * (t + 1)],
                rhs=x_codes[:, 2 * first : 2 * (first + width)].bitcast(FP4X4),
                rhs_scale=x_plane[:, first : first + width],
                start=True,
                stop=True,
            )

        def entries(first, width):
            return offsets[:, first // LANES : (first + width) // LANES]

        def row(t):
            return (t + 1) % PACK

        def look_up(t, first, width):
            nc.vector.tensor_copy(old[:, row(t), first : first + width], store[t][:].indirect(entries(first, width)))

        def look_up_on_scalar(t, first, width):
            nc.scalar.activation(old[:, row(t), first : first + width], store[t][:].indirect(entries(first, width)), ACT.Copy)

        def quarters(rows, parts):
            flat = rows.rearrange("p t (q c) -> p (t q) c", c=QUARTER)
            start, stop = (PACK * row(t) + quarter for t, quarter in (parts[0], parts[-1]))
            return flat[:, start : stop + 1 : max(stop - start, 1), :]

        def smaller(bank, one, other):
            parts = sorted({one, other}, key=lambda part: (row(part[0]), part[1]))
            y = psum.tile([P, len(parts), QUARTER], F32, name="bank%d" % bank)
            for i, (t, quarter) in enumerate(parts):
                project(y[:, i, :], t, quarter * QUARTER, QUARTER)
            nc.vector.tensor_tensor(quarters(new, parts), quarters(old[:], parts), y[:], ALU.min)

        def put_back(t, first, width):
            nc.vector.tensor_copy(store[t][:].indirect(entries(first, width)), new[:, row(t), first : first + width])

        def put_back_on_scalar(t, first, width):
            nc.scalar.activation(store[t][:].indirect(entries(first, width)), new[:, row(t), first : first + width], ACT.Copy)

        def hand_out(t):
            nc.sync.dma_start(out_rows[:, t, :], store[t][:])

        look_up(0, 0, QUARTER)
        look_up(0, QUARTER, FIRST_ON_VECTOR - QUARTER)
        look_up_on_scalar(0, FIRST_ON_VECTOR, T - FIRST_ON_VECTOR)
        smaller(0, (0, 0), (0, 0))
        smaller(1, (0, 1), (0, 2))
        put_back_on_scalar(0, 0, 256)
        put_back_on_scalar(0, 256, 384)
        look_up(1, 0, BANK)
        look_up(1, BANK, BANK)
        smaller(2, (0, 3), (1, 0))
        put_back_on_scalar(1, 0, 256)
        put_back_on_scalar(0, 640, 384)
        hand_out(0)
        look_up(2, 0, T - QUARTER)
        look_up(2, T - QUARTER, QUARTER)
        smaller(3, (1, 2), (2, 0))
        smaller(4, (1, 1), (2, 1))
        nc.vector.tensor_tensor(store[1][:].indirect(entries(640, SLIVER)), new[:, row(1), 640 : 640 + SLIVER], nothing[:], ALU.add)
        put_back_on_scalar(1, 256, 384)
        look_up(3, 0, T - QUARTER)
        look_up(3, T - QUARTER, QUARTER)
        smaller(5, (1, 3), (3, 0))
        smaller(6, (2, 2), (3, 1))
        smaller(7, (2, 3), (3, 2))
        smaller(0, (3, 3), (3, 3))
        put_back(2, 0, T)
        put_back_on_scalar(3, 0, 256)
        put_back_on_scalar(1, 640 + SLIVER, 384 - SLIVER)
        hand_out(1)
        hand_out(2)
        put_back_on_scalar(3, 256, 384)
        put_back_on_scalar(3, 640, 384)
        hand_out(3)

        pair_words = shared[:, : 2 * U]
        pairs = pair_words.bitcast(BF16).rearrange("p (h c e) -> p h c e", h=2, e=2)
        for t in range(2):
            nc.gpsimd.tensor_scalar(pairs[:, 0, :, t], store[t][:], 1.0, -0.0, ALU.mult, ALU.add)
        own = slice(U - OWN, U)
        nc.vector.tensor_copy(pairs[:, 1, : U - OWN, 0], store[2][:, : U - OWN])
        nc.scalar.copy(pairs[:, 1, own, 0], store[2][:, own])
        nc.scalar.copy(pairs[:, 1, own, 1], store[3][:, own])
        for first, width in PAIR_CHUNKS:
            nc.vector.tensor_copy(pairs[:, 1, first : first + width, 1], store[3][:, first : first + width])
        words = keep.tile([P, U], U32, name="words", align_bytes=64)
        plane = keep.tile([P, GROUP], U8, name="plane", align_bytes=64)
        woven = keep.tile([P, U - OWN, PACK], BF16, name="woven", align_bytes=64)

        def room(first):
            return first % (U - OWN)

        def weave(first, width, on_vector):
            view = I32 if on_vector else U32
            source = pair_words.bitcast(view).rearrange("p (h c) -> p c h", h=2)[:, first : first + width, :]
            target = woven[:, room(first) : room(first) + width].rearrange("p c t -> p (c t)").bitcast(view).rearrange("p (c h) -> p c h", h=2)
            if on_vector:
                nc.vector.tensor_copy(target, source)
            else:
                nc.scalar.copy(target, source)

        def quantise(first, width):
            group, col = divmod(first, GROUP)
            nc.vector.quantize_mx(
                out=words[:, first : first + width].bitcast(FP8X4),
                scales=plane[4 * group :, col : col + width],
                in_=woven[:, room(first) : room(first) + width].rearrange("p c t -> p (c t)"),
            )

        def store_words(first, width):
            nc.sync.dma_start(out_words[:, first : first + width], words[:, first : first + width].bitcast(I32))

        for first, width in SCALAR_WEAVES:
            weave(first, width, False)
        weave(512, 384, True)
        quantise(0, 256)
        quantise(256, 256)
        quantise(512, 256)
        store_words(0, 768)
        weave(1792, 128, False)
        weave(1920, 128, False)
        quantise(768, 256)
        quantise(1024, 256)
        quantise(1280, 256)
        store_words(768, 768)
        quantise(1536, 256)
        quantise(1792, 128)
        quantise(1920, 128)
        store_words(1536, 512)
        for q in range(QUADRANTS):
            nc.scalar.dma_start(
                out_2[0, 4 * q : 4 * q + 4, :].bitcast(I32).rearrange("r (g c) -> g r c", g=U // GROUP),
                plane[32 * q : 32 * q + 4 * (U // GROUP), :].bitcast(I32),
            )
